import numpy as np
import ml_dtypes


def mxq(x, axis, fmt="e4m3"):
    dtype, down = {"e4m3": (ml_dtypes.float8_e4m3fn, 7), "e5m2": (ml_dtypes.float8_e5m2, 14)}[fmt]
    v = np.moveaxis(np.asarray(x, np.float32).astype(ml_dtypes.bfloat16).astype(np.float64), axis, -1)
    blocks = v.reshape(v.shape[:-1] + (-1, 32))
    amax = np.abs(blocks).max(-1, keepdims=True)
    byte = np.maximum(np.where(amax > 0, np.frexp(amax)[1] - 1 + 127, 0) - down, 1)
    scale = np.exp2(byte - 127.0)
    codes = (blocks / scale).astype(np.float32).astype(dtype).astype(np.float64)
    return np.moveaxis((codes * scale).reshape(v.shape), -1, axis)


WIDE = False


def mx_kscale(k):
    if not WIDE:
        return np.ones(k)
    levels = np.array([10, -10, 5, -5, 0])
    if k % 512:
        return np.exp2(np.random.permutation(np.resize(levels, k // 32))).repeat(32)
    a = np.empty((k // 512, 16))
    for p in range(k // 512):
        a[p, :8] = np.random.permutation(np.resize(levels, 8))
        for g in range(8):
            far = levels[np.abs(levels - a[p, g]) >= 10]
            a[p, g + 8] = far[np.random.randint(len(far))]
    return np.exp2(a.ravel()).repeat(32)


def f64(x):
    return np.asarray(x).astype(np.float64)


def striped(idx):
    return np.tile(idx.reshape(-1, 16).T, (8, 1)).astype(np.uint16)


def unstriped(offs):
    return offs[:16].T.reshape(-1).astype(np.int64)


E2M1 = np.array([0.0, 0.5, 1.0, 1.5, 2.0, 3.0, 4.0, 6.0, -0.0, -0.5, -1.0, -1.5, -2.0, -3.0, -4.0, -6.0])


def pack_weight(w, fmt):
    k, n = w.shape
    w = f64(np.asarray(w, np.float32).astype(ml_dtypes.bfloat16)).reshape(k // 32, 32, n)
    amax = np.abs(w).max(1)
    if fmt == "e4m3":
        byte = np.frexp(amax)[1] - 1 + 127 - 7
    else:
        mant, ex = np.frexp(amax / 6.0)
        byte = np.where(mant > 0.5, ex, ex - 1) + 127
    byte = np.clip(np.where(amax > 0, byte, 1), 1, 254)
    scaled = (w * np.exp2(127.0 - byte)[:, None, :]).reshape(k, n).astype(np.float32)
    by_word = np.ascontiguousarray(scaled.reshape(k // 512, 128, 4, n).transpose(0, 1, 3, 2))
    if fmt == "e4m3":
        words = by_word.astype(ml_dtypes.float8_e4m3fn).view(np.uint8)
    else:
        c = by_word.astype(ml_dtypes.float4_e2m1fn).view(np.uint8) & 0xF
        words = (c[..., 0::2] | (c[..., 1::2] << 4)).reshape(k // 512, 128, 2 * n)
    return np.ascontiguousarray(words), np.ascontiguousarray(byte.astype(np.uint8).reshape(k // 512, 16, n))


def unpack_weight(words, scales, fmt):
    g, _, n = scales.shape
    words = np.ascontiguousarray(words).reshape(g, 128, n, -1)
    if fmt == "e4m3":
        vals = words.view(ml_dtypes.float8_e4m3fn).astype(np.float64)
    else:
        nib = np.empty((g, 128, n, 4), np.uint8)
        nib[..., 0::2] = words & 0xF
        nib[..., 1::2] = words >> 4
        vals = E2M1[nib]
    vals = vals * np.repeat(np.exp2(scales.astype(np.float64) - 127.0), 8, axis=1)[..., None]
    return vals.transpose(0, 1, 3, 2).reshape(g * 512, n)


def gelu(v):
    return 0.5 * v * (1.0 + np.tanh(np.sqrt(2.0 / np.pi) * (v + 0.044715 * v**3)))


def striped8(idx):
    return np.concatenate([v.reshape(-1, 16).T for v in idx]).astype(np.uint16)


def unstriped8(offs):
    return np.stack([offs[16 * g:16 * g + 16].T.reshape(-1) for g in range(8)]).astype(np.int64)


def runs(v, idx8):
    k = np.arange(v.shape[0])
    return v[k[:, None], idx8[k % 512 // 64]]


def put_heads(h, wgs, idx8, t2):
    r = np.arange(h.shape[0])
    page = np.zeros((h.shape[0], t2))
    page[r[:, None], idx8[r % 512 // 64]] = wgs[r // 4 % 128] * h
    return page


K, H, N, T, S, T2 = 1024, 1024, 512, 2048, 1024, 2048


def setup_inputs():
    n = np.random.standard_normal
    s = mx_kscale(K)[:, None]
    u = mx_kscale(H)[:, None]
    tab_words, tab_scales = pack_weight(n((K, T)) * s, "e4m3")
    wb_words, wb_scales = pack_weight(0.5 * n((K, H)) / np.sqrt(K) / s, "e2m1")
    return {
        "tab_words": tab_words, "tab_scales": tab_scales,
        "offs": striped8(np.stack([np.random.permutation(T)[:S] for _ in range(8)])),
        "wa": (0.5 * n((K, H)) / np.sqrt(K) / s).astype(np.float32),
        "wb_words": wb_words, "wb_scales": wb_scales,
        "gain": (np.exp(0.3 * n(H)) * u[:, 0]).astype(np.float32),
        "wc": (1.2 * n((H, N)) / np.sqrt(H) / u).astype(np.float32),
        "offs2": striped8(np.stack([np.random.permutation(T2)[:S] for _ in range(8)])),
        "wgo": np.repeat(np.random.uniform(0.5, 2.0, (8, S)), 16, axis=0).astype(np.float32),
    }


def reference(tab_words, tab_scales, offs, wa, wb_words, wb_scales, gain, wc, offs2, wgo):
    v = runs(unpack_weight(tab_words, tab_scales, "e4m3"), unstriped8(offs))
    a = mxq(f64(wa), 0, "e4m3").T @ v
    b = unpack_weight(wb_words, wb_scales, "e2m1").T @ v
    h = f64(gain)[:, None] * (np.exp(a) - np.exp(b))
    hq = mxq(h, 0, "e4m3")
    c = mxq(f64(wc), 0, "e4m3").T @ hq
    y = np.log1p(np.square(c))
    out = put_heads(y, f64(wgo), unstriped8(offs2), T2)
    return out

@@ -1,0 +1,302 @@
+from contextlib import ExitStack
+
+import concourse.mybir as mybir
+
+K, H, N, T, S, T2 = 1024, 1024, 512, 2048, 1024, 2048
+FLOPS = 2 * (2 * K * H * S + H * N * S)
+
+F32 = mybir.dt.float32
+BF16 = mybir.dt.bfloat16
+I32 = mybir.dt.int32
+U32 = mybir.dt.uint32
+U16 = mybir.dt.uint16
+U8 = mybir.dt.uint8
+E4M3 = mybir.dt.float8_e4m3fn_x4
+E2M1 = mybir.dt.float4_e2m1fn_x4
+ACT = mybir.ActivationFunctionType
+ALU = mybir.AluOpType
+
+P = 128
+PASSES = 2
+BLK = 128
+GRP = 256
+GROUPS = S // GRP
+
+
+def tile_list_baggage_density_cues_kernel(
+    tc, tab_words, tab_scales, offs, wa, wb_words, wb_scales, gain, wc, offs2, wgo, out
+):
+    nc = tc.nc
+    with ExitStack() as ctx:
+        lists = ctx.enter_context(tc.tile_pool(name="lists", bufs=1))
+        keep = ctx.enter_context(tc.tile_pool(name="keep", bufs=1))
+        stage = ctx.enter_context(tc.tile_pool(name="stage", bufs=2))
+        exps = ctx.enter_context(tc.tile_pool(name="exps", bufs=6))
+        ps_ab = ctx.enter_context(tc.psum_pool(name="ps_ab", bufs=3))
+        ps_c = ctx.enter_context(tc.psum_pool(name="ps_c", bufs=2))
+
+        def held(name, shape, dtype):
+            return keep.tile(shape, dtype, name=name, align_bytes=64)
+
+        pick = lists.tile([P, S // 16], U16, name="pick")
+        place = lists.tile([P, S // 16], U16, name="place")
+
+        tscale = held("tscale", [P, T], U8)
+        wbs_raw = held("wbs_raw", [P, PASSES * H], U8)
+        vplanes = held("vplanes", [P, PASSES * S], U8)
+        nc.vector.memset(tscale[:].bitcast(I32), 0)
+        nc.vector.memset(wbs_raw[:].bitcast(I32), 0)
+        nc.vector.memset(vplanes[:].bitcast(I32), 0)
+
+        def reused(name, tag, shape, dtype):
+            return keep.tile(shape, dtype, name=name, tag=tag, align_bytes=64)
+
+        warm = held("warm", [P, 1], F32)
+        nc.gpsimd.memset(warm[:], 0.0)
+        nc.scalar.activation(warm[:], warm[:], ACT.Exp)
+        nc.sync.dma_start(pick[:], offs)
+        nc.sync.dma_start(place[:], offs2)
+        nc.sync.dma_start(
+            out=tscale[0:P:4, :].bitcast(I32), in_=tab_scales.bitcast(I32).rearrange("a q t -> q a t")
+        )
+        wa_raw = {}
+
+        def load_wa(a, b):
+            wa_raw[a, b] = reused(f"wa_raw{a}{b}", f"wa{a}", [P, 4, 512], F32)
+            nc.sync.dma_start(
+                out=wa_raw[a, b][:],
+                in_=wa[512 * a : 512 * (a + 1), 512 * b : 512 * (b + 1)].rearrange("(p i) c -> p i c", i=4),
+            )
+
+        twords = [reused(f"twords{a}", f"tab{a}", [P, T], U32) for a in range(PASSES)]
+
+        def load_twords(a):
+            nc.sync.dma_start(
+                out=twords[a][:].bitcast(I32),
+                in_=tab_words[a].rearrange("p t i -> p (t i)").bitcast(I32),
+            )
+
+        load_wa(0, 0)
+        wbs_rows = wb_scales.rearrange("a (d r) c -> r d a c", r=4)
+        for r in range(4):
+            nc.sync.dma_start(
+                out=wbs_raw[r:P:32, :].bitcast(I32).rearrange("d (a c) -> d a c", a=PASSES),
+                in_=wbs_rows[r].bitcast(I32),
+            )
+        load_twords(0)
+        load_wa(1, 0)
+        wbw_raw = reused("wbw_raw", "wb_in", [P, PASSES, H // 2], I32)
+        nc.sync.dma_start(out=wbw_raw[:], in_=wb_words.bitcast(I32).rearrange("a p c -> p a c"))
+        load_twords(1)
+
+        gain_span = held("gain_span", [P, PASSES, 13], F32)
+        gain_rows = gain.rearrange("(b m x) -> m b x", b=PASSES, x=16)
+        for u in range(4):
+            nc.gpsimd.dma_start(out=gain_span[u:P:4, :, :], in_=gain_rows[:, :, u : u + 13])
+        gains = held("gains", [P, PASSES, 4], F32)
+        nc.gpsimd.tensor_copy(gains[:], gain_span[:, :, 0:13:4])
+
+        gscale = held("gscale", [P, S], U8)
+        nc.vector.tensor_copy(gscale[:], tscale[:].indirect(pick[:]))
+        for d in range(4):
+            nc.scalar.dma_start(
+                out=vplanes[32 * d : 32 * d + 4, :].bitcast(I32),
+                in_=gscale[32 * d : 32 * (d + 1) : 4, :].bitcast(I32),
+            )
+        vwords = {}
+        for half in range(2):
+            for a in range(PASSES):
+                vwords[a, half] = held(f"vwords{a}{half}", [P, 512], U32)
+                nc.vector.tensor_copy(
+                    vwords[a, half][:], twords[a][:].indirect(pick[:, 32 * half : 32 * (half + 1)])
+                )
+
+        wbw = held("wbw", [P, PASSES * H // 2], I32)
+        nc.vector.tensor_copy(
+            wbw[:].rearrange("p (a t m u) -> p a t m u", a=PASSES, t=4, u=2),
+            wbw_raw[:].rearrange("p a (m t u) -> p a t m u", t=4, u=2),
+        )
+        wbs = held("wbs", [P, PASSES * H], U8)
+        nc.vector.tensor_copy(
+            wbs[:].bitcast(I32).rearrange("p (a t m) -> p a t m", a=PASSES, t=4),
+            wbs_raw[:].bitcast(I32).rearrange("p (a m t) -> p a t m", a=PASSES, t=4),
+        )
+        wbw_bytes = wbw[:].bitcast(U8)
+
+        wa_q, wa_s = {}, {}
+
+        def prep_wa(a, b):
+            rounded = stage.tile([P, 2048], BF16, name="wa_bf", align_bytes=64)
+            nc.scalar.copy(
+                rounded[:].rearrange("p (t m u i) -> p t m i u", t=4, u=4, i=4),
+                wa_raw[a, b][:].rearrange("p i (m t u) -> p t m i u", t=4, u=4),
+            )
+            wa_q[a, b] = held(f"wa_q{a}{b}", [P, 512], U32)
+            wa_s[a, b] = held(f"wa_s{a}{b}", [P, 512], U8)
+            nc.vector.quantize_mx(out=wa_q[a, b][:].bitcast(E4M3), scales=wa_s[a, b][:], in_=rounded[:])
+
+        wc_q, wc_s = {}, {}
+
+        def prep_wc(b):
+            rounded = stage.tile([P, 2048], BF16, name="wc_bf", align_bytes=64)
+            nc.vector.tensor_copy(
+                rounded[:].rearrange("p (i q t) -> p q t i", i=4, t=4),
+                wc_raw[b][:].rearrange("p t (q i) -> p q t i", i=4),
+            )
+            wc_q[b] = held(f"wc_q{b}", [P, N], U32)
+            wc_s[b] = held(f"wc_s{b}", [P, N], U8)
+            nc.vector.quantize_mx(out=wc_q[b][:].bitcast(E4M3), scales=wc_s[b][:], in_=rounded[:])
+
+        ea, eb, hb, h_q, h_s = {}, {}, {}, {}, {}
+
+        def readings(b, g):
+            if (b, g) == (1, GROUPS - 2):
+                ea[b, g] = keep.tile([P, 4 * GRP], F32, name="ea_late", tag="late", align_bytes=64)
+            else:
+                ea[b, g] = exps.tile([P, 4 * GRP], F32, name="ea", align_bytes=64)
+            eb[b, g] = exps.tile([P, 4 * GRP], F32, name="eb", align_bytes=64)
+            for s in range(GRP // BLK):
+                j0 = g * GRP + s * BLK
+                half, c0 = divmod(j0, 512)
+                bank_a = ps_ab.tile([P, 4, BLK], F32, name="bank_a")
+                bank_b = ps_ab.tile([P, 4, BLK], F32, name="bank_b")
+                for t in range(4):
+                    for a in range(PASSES):
+                        nc.tensor.matmul_mx(
+                            out=bank_a[:, t, :],
+                            lhsT=wa_q[a, b][:, P * t : P * (t + 1)].bitcast(E4M3),
+                            lhsT_scale=wa_s[a, b][:, P * t : P * (t + 1)],
+                            rhs=vwords[a, half][:, c0 : c0 + BLK].bitcast(E4M3),
+                            rhs_scale=vplanes[:, a * S + j0 : a * S + j0 + BLK],
+                            start=(a == 0),
+                            stop=(a == PASSES - 1),
+                        )
+                nc.scalar.activation(
+                    ea[b, g][:, 4 * BLK * s : 4 * BLK * (s + 1)].rearrange("p (j t) -> p j t", t=4),
+                    bank_a[:].rearrange("p t j -> p j t"),
+                    ACT.Exp,
+                )
+                for t in range(4):
+                    for a in range(PASSES):
+                        col = a * H + t * 256 + b * P
+                        nc.tensor.matmul_mx(
+                            out=bank_b[:, t, :],
+                            lhsT=wbw_bytes[:, 2 * col : 2 * (col + P)].bitcast(E2M1),
+                            lhsT_scale=wbs[:, col : col + P],
+                            rhs=vwords[a, half][:, c0 : c0 + BLK].bitcast(E4M3),
+                            rhs_scale=vplanes[:, a * S + j0 : a * S + j0 + BLK],
+                            start=(a == 0),
+                            stop=(a == PASSES - 1),
+                        )
+                nc.scalar.activation(
+                    eb[b, g][:, 4 * BLK * s : 4 * BLK * (s + 1)].rearrange("p (j t) -> p j t", t=4),
+                    bank_b[:].rearrange("p t j -> p j t"),
+                    ACT.Exp,
+                )
+
+        diff = {}
+
+        def subtract(b, g):
+            diff[b, g] = stage.tile([P, 4 * GRP], F32, name="diff", align_bytes=64)
+            nc.vector.tensor_tensor(diff[b, g][:], ea[b, g][:], eb[b, g][:], ALU.subtract)
+
+        def scale(b, g):
+            hb[b, g] = stage.tile([P, 4 * GRP], BF16, name="hb", align_bytes=64)
+            nc.vector.tensor_tensor(
+                hb[b, g][:].rearrange("p (j t) -> p j t", t=4),
+                diff[b, g][:].rearrange("p (j t) -> p j t", t=4),
+                gains[:, b, :].unsqueeze(1).to_broadcast([P, GRP, 4]),
+                ALU.mult,
+            )
+
+        def quantise(b, g):
+            h_q[b, g] = held(f"h_q{b}{g}", [P, GRP], U32)
+            h_s[b, g] = held(f"h_s{b}{g}", [P, GRP], U8)
+            nc.vector.quantize_mx(out=h_q[b, g][:].bitcast(E4M3), scales=h_s[b, g][:], in_=hb[b, g][:])
+
+        sq_first = held("sq_first", [P, 4, GRP], F32)
+        y_rest = held("y_rest", [P, 4, S - GRP], F32)
+
+        def mix(g):
+            for pair in range(2):
+                bank = ps_c.tile([P, 2, GRP], F32, name="bank_c")
+                for e in range(2):
+                    i = 2 * pair + e
+                    for b in range(PASSES):
+                        nc.tensor.matmul_mx(
+                            out=bank[:, e, :],
+                            lhsT=wc_q[b][:, P * i : P * (i + 1)].bitcast(E4M3),
+                            lhsT_scale=wc_s[b][:, P * i : P * (i + 1)],
+                            rhs=h_q[b, g][:].bitcast(E4M3),
+                            rhs_scale=h_s[b, g][:],
+                            start=(b == 0),
+                            stop=(b == PASSES - 1),
+                        )
+                if g == 0:
+                    dst = sq_first[:, 2 * pair : 2 * pair + 2, :]
+                else:
+                    dst = y_rest[:, 2 * pair : 2 * pair + 2, (g - 1) * GRP : g * GRP]
+                nc.scalar.activation(dst, bank[:], ACT.Square)
+
+        units = [(b, g) for b in range(PASSES) for g in range(GROUPS)]
+        prep_wa(0, 0)
+        prep_wa(1, 0)
+        load_wa(0, 1)
+        load_wa(1, 1)
+        wc_raw = [reused(f"wc_raw{b}", f"tab{b}", [P, 4, N], F32) for b in range(PASSES)]
+        for b in range(PASSES):
+            rows = wc[512 * b : 512 * (b + 1), :].rearrange("(m t u) n -> t m u n", t=4, u=4)
+            for t in range(4):
+                nc.sync.dma_start(out=wc_raw[b][:, t, :], in_=rows[t])
+        weights = reused("weights", "wb_in", [P, S], F32)
+        nc.sync.dma_start(out=weights[:], in_=wgo)
+        for k in range(len(units) + 2):
+            if k < len(units):
+                readings(*units[k])
+                subtract(*units[k])
+            if k == 0:
+                prep_wa(0, 1)
+            if k == 1:
+                prep_wa(1, 1)
+            if k in (3, 4):
+                prep_wc(k - 3)
+            if 1 <= k <= len(units):
+                scale(*units[k - 1])
+            if k >= 2:
+                quantise(*units[k - 2])
+                if units[k - 2] == (PASSES - 1, 0):
+                    mix(0)
+
+        pages = [held(f"page{i}", [P, T2], F32) for i in range(4)]
+        for i in range(4):
+            for half in range(2):
+                nc.vector.memset(pages[i][:, 1024 * half : 1024 * (half + 1)], 0.0)
+
+        y_first = keep.tile([P, 4 * GRP], F32, name="y_first", tag="late", align_bytes=64)
+        for pair in range(2):
+            nc.scalar.activation(
+                y_first[:, 2 * GRP * pair : 2 * GRP * (pair + 1)],
+                sq_first[:, 2 * pair : 2 * pair + 2, :].rearrange("p i j -> p (i j)"),
+                ACT.Ln,
+                bias=1.0,
+            )
+        for g in range(1, GROUPS):
+            mix(g)
+        for i in range(4):
+            nc.scalar.activation(y_rest[:, i, :], y_rest[:, i, :], ACT.Ln, bias=1.0)
+        for i in range(4):
+            nc.vector.tensor_tensor(
+                pages[i][:].indirect(place[:, 0 : GRP // 16]),
+                y_first[:, GRP * i : GRP * (i + 1)],
+                weights[:, 0:GRP],
+                ALU.mult,
+            )
+        rows = out.rearrange("(p i) t -> i p t", i=4)
+        for i in range(4):
+            nc.vector.tensor_tensor(
+                pages[i][:].indirect(place[:, GRP // 16 : S // 16]),
+                y_rest[:, i, :],
+                weights[:, GRP:S],
+                ALU.mult,
+            )
+            nc.sync.dma_start(out=rows[i], in_=pages[i][:])

@@ -21,6 +21,7 @@ PASSES = 2
 BLK = 128
 GRP = 256
 GROUPS = S // GRP
+HALF = S // 2
 
 
 def tile_list_baggage_density_cues_kernel(
@@ -31,9 +32,8 @@ def tile_list_baggage_density_cues_kernel(
         lists = ctx.enter_context(tc.tile_pool(name="lists", bufs=1))
         keep = ctx.enter_context(tc.tile_pool(name="keep", bufs=1))
         stage = ctx.enter_context(tc.tile_pool(name="stage", bufs=2))
-        exps = ctx.enter_context(tc.tile_pool(name="exps", bufs=6))
-        ps_ab = ctx.enter_context(tc.psum_pool(name="ps_ab", bufs=3))
-        ps_c = ctx.enter_context(tc.psum_pool(name="ps_c", bufs=2))
+        exps = ctx.enter_context(tc.tile_pool(name="exps", bufs=5))
+        banks = ctx.enter_context(tc.psum_pool(name="banks", bufs=8))
 
         def held(name, shape, dtype):
             return keep.tile(shape, dtype, name=name, align_bytes=64)
@@ -44,15 +44,15 @@ def tile_list_baggage_density_cues_kernel(
         tscale = held("tscale", [P, T], U8)
         wbs_raw = held("wbs_raw", [P, PASSES * H], U8)
         vplanes = held("vplanes", [P, PASSES * S], U8)
-        nc.vector.memset(tscale[:].bitcast(I32), 0)
-        nc.vector.memset(wbs_raw[:].bitcast(I32), 0)
-        nc.vector.memset(vplanes[:].bitcast(I32), 0)
+        nc.gpsimd.memset(tscale[:].bitcast(I32), 0)
+        nc.gpsimd.memset(wbs_raw[:].bitcast(I32), 0)
+        nc.gpsimd.memset(vplanes[:].bitcast(I32), 0)
 
         def reused(name, tag, shape, dtype):
             return keep.tile(shape, dtype, name=name, tag=tag, align_bytes=64)
 
         warm = held("warm", [P, 1], F32)
-        nc.gpsimd.memset(warm[:], 0.0)
+        nc.vector.memset(warm[:], 0.0)
         nc.scalar.activation(warm[:], warm[:], ACT.Exp)
         nc.sync.dma_start(pick[:], offs)
         nc.sync.dma_start(place[:], offs2)
@@ -99,7 +99,7 @@ def tile_list_baggage_density_cues_kernel(
         gscale = held("gscale", [P, S], U8)
         nc.vector.tensor_copy(gscale[:], tscale[:].indirect(pick[:]))
         for d in range(4):
-            nc.scalar.dma_start(
+            nc.sync.dma_start(
                 out=vplanes[32 * d : 32 * d + 4, :].bitcast(I32),
                 in_=gscale[32 * d : 32 * (d + 1) : 4, :].bitcast(I32),
             )
@@ -127,7 +127,7 @@ def tile_list_baggage_density_cues_kernel(
 
         def prep_wa(a, b):
             rounded = stage.tile([P, 2048], BF16, name="wa_bf", align_bytes=64)
-            nc.scalar.copy(
+            (nc.scalar.copy if b == 0 else nc.vector.tensor_copy)(
                 rounded[:].rearrange("p (t m u i) -> p t m i u", t=4, u=4, i=4),
                 wa_raw[a, b][:].rearrange("p i (m t u) -> p t m i u", t=4, u=4),
             )
@@ -138,8 +138,8 @@ def tile_list_baggage_density_cues_kernel(
         wc_q, wc_s = {}, {}
 
         def prep_wc(b):
-            rounded = stage.tile([P, 2048], BF16, name="wc_bf", align_bytes=64)
-            nc.vector.tensor_copy(
+            rounded = reused(f"wc_bf{b}", f"then{b + 2}", [P, 2048], BF16)
+            nc.scalar.copy(
                 rounded[:].rearrange("p (i q t) -> p q t i", i=4, t=4),
                 wc_raw[b][:].rearrange("p t (q i) -> p q t i", i=4),
             )
@@ -150,16 +150,16 @@ def tile_list_baggage_density_cues_kernel(
         ea, eb, hb, h_q, h_s = {}, {}, {}, {}, {}
 
         def readings(b, g):
-            if (b, g) == (1, GROUPS - 2):
-                ea[b, g] = keep.tile([P, 4 * GRP], F32, name="ea_late", tag="late", align_bytes=64)
+            if b == 0 and g > 0:
+                ea[b, g] = reused(f"ea0{g}", f"then{g}", [P, 4 * GRP], F32)
             else:
                 ea[b, g] = exps.tile([P, 4 * GRP], F32, name="ea", align_bytes=64)
             eb[b, g] = exps.tile([P, 4 * GRP], F32, name="eb", align_bytes=64)
             for s in range(GRP // BLK):
                 j0 = g * GRP + s * BLK
                 half, c0 = divmod(j0, 512)
-                bank_a = ps_ab.tile([P, 4, BLK], F32, name="bank_a")
-                bank_b = ps_ab.tile([P, 4, BLK], F32, name="bank_b")
+                bank_a = banks.tile([P, 4, BLK], F32, name="bank_a", tag="bank")
+                bank_b = banks.tile([P, 4, BLK], F32, name="bank_b", tag="bank")
                 for t in range(4):
                     for a in range(PASSES):
                         nc.tensor.matmul_mx(
@@ -214,12 +214,12 @@ def tile_list_baggage_density_cues_kernel(
             h_s[b, g] = held(f"h_s{b}{g}", [P, GRP], U8)
             nc.vector.quantize_mx(out=h_q[b, g][:].bitcast(E4M3), scales=h_s[b, g][:], in_=hb[b, g][:])
 
-        sq_first = held("sq_first", [P, 4, GRP], F32)
-        y_rest = held("y_rest", [P, 4, S - GRP], F32)
+        chunks = ((0,), (1,), (2, 3))
+        ys = [held(f"y{c}", [P, 4, GRP * len(gs)], F32) for c, gs in enumerate(chunks)]
 
-        def mix(g):
-            for pair in range(2):
-                bank = ps_c.tile([P, 2, GRP], F32, name="bank_c")
+        def mix(g, pair, y, at):
+            if True:
+                bank = banks.tile([P, 2, GRP], F32, name="bank_c", tag="bank")
                 for e in range(2):
                     i = 2 * pair + e
                     for b in range(PASSES):
@@ -232,10 +232,7 @@ def tile_list_baggage_density_cues_kernel(
                             start=(b == 0),
                             stop=(b == PASSES - 1),
                         )
-                if g == 0:
-                    dst = sq_first[:, 2 * pair : 2 * pair + 2, :]
-                else:
-                    dst = y_rest[:, 2 * pair : 2 * pair + 2, (g - 1) * GRP : g * GRP]
+                dst = y[:, 2 * pair : 2 * pair + 2, at * GRP : (at + 1) * GRP]
                 nc.scalar.activation(dst, bank[:], ACT.Square)
 
         units = [(b, g) for b in range(PASSES) for g in range(GROUPS)]
@@ -243,60 +240,51 @@ def tile_list_baggage_density_cues_kernel(
         prep_wa(1, 0)
         load_wa(0, 1)
         load_wa(1, 1)
-        wc_raw = [reused(f"wc_raw{b}", f"tab{b}", [P, 4, N], F32) for b in range(PASSES)]
-        for b in range(PASSES):
+        wc_raw = {}
+
+        def load_wc(b):
+            wc_raw[b] = reused(f"wc_raw{b}", f"wa{b}", [P, 4, N], F32)
             rows = wc[512 * b : 512 * (b + 1), :].rearrange("(m t u) n -> t m u n", t=4, u=4)
             for t in range(4):
                 nc.sync.dma_start(out=wc_raw[b][:, t, :], in_=rows[t])
-        weights = reused("weights", "wb_in", [P, S], F32)
-        nc.sync.dma_start(out=weights[:], in_=wgo)
+
         for k in range(len(units) + 2):
+            if k in (0, 1):
+                prep_wa(k, 1)
+                load_wc(k)
             if k < len(units):
                 readings(*units[k])
                 subtract(*units[k])
-            if k == 0:
-                prep_wa(0, 1)
             if k == 1:
-                prep_wa(1, 1)
-            if k in (3, 4):
-                prep_wc(k - 3)
+                weights = reused("weights", "then1", [P, S], F32)
+                nc.sync.dma_start(out=weights[:], in_=wgo)
+            if k in (4, 5):
+                prep_wc(k - 4)
             if 1 <= k <= len(units):
                 scale(*units[k - 1])
             if k >= 2:
                 quantise(*units[k - 2])
-                if units[k - 2] == (PASSES - 1, 0):
-                    mix(0)
 
         pages = [held(f"page{i}", [P, T2], F32) for i in range(4)]
-        for i in range(4):
+        for i in range(2):
             for half in range(2):
                 nc.vector.memset(pages[i][:, 1024 * half : 1024 * (half + 1)], 0.0)
+        for i in range(2, 4):
+            for part in range(4):
+                nc.gpsimd.memset(pages[i][:, 512 * part : 512 * (part + 1)], 0.0)
 
-        y_first = keep.tile([P, 4 * GRP], F32, name="y_first", tag="late", align_bytes=64)
-        for pair in range(2):
-            nc.scalar.activation(
-                y_first[:, 2 * GRP * pair : 2 * GRP * (pair + 1)],
-                sq_first[:, 2 * pair : 2 * pair + 2, :].rearrange("p i j -> p (i j)"),
-                ACT.Ln,
-                bias=1.0,
-            )
-        for g in range(1, GROUPS):
-            mix(g)
-        for i in range(4):
-            nc.scalar.activation(y_rest[:, i, :], y_rest[:, i, :], ACT.Ln, bias=1.0)
-        for i in range(4):
-            nc.vector.tensor_tensor(
-                pages[i][:].indirect(place[:, 0 : GRP // 16]),
-                y_first[:, GRP * i : GRP * (i + 1)],
-                weights[:, 0:GRP],
-                ALU.mult,
-            )
+        for gs, y in zip(chunks, ys):
+            for pair in range(2):
+                for at, g in enumerate(gs):
+                    mix(g, pair, y, at)
+                both = y[:, 2 * pair : 2 * pair + 2, :]
+                nc.scalar.activation(both, both, ACT.Ln, bias=1.0)
         rows = out.rearrange("(p i) t -> i p t", i=4)
-        for i in range(4):
-            nc.vector.tensor_tensor(
-                pages[i][:].indirect(place[:, GRP // 16 : S // 16]),
-                y_rest[:, i, :],
-                weights[:, GRP:S],
-                ALU.mult,
-            )
-            nc.sync.dma_start(out=rows[i], in_=pages[i][:])
+        for gs, y in zip(chunks, ys):
+            j0, j1 = GRP * gs[0], GRP * (gs[-1] + 1)
+            for i in range(4):
+                nc.vector.tensor_tensor(
+                    pages[i][:].indirect(place[:, j0 // 16 : j1 // 16]), y[:, i, :], weights[:, j0:j1], ALU.mult
+                )
+                if j1 == S:
+                    nc.sync.dma_start(out=rows[i], in_=pages[i][:])

@@ -18,10 +18,8 @@ ALU = mybir.AluOpType
 
 P = 128
 PASSES = 2
-BLK = 128
-GRP = 256
-GROUPS = S // GRP
 HALF = S // 2
+QUART = S // 4
 
 
 def tile_list_baggage_density_cues_kernel(
@@ -30,261 +28,307 @@ def tile_list_baggage_density_cues_kernel(
     nc = tc.nc
     with ExitStack() as ctx:
         lists = ctx.enter_context(tc.tile_pool(name="lists", bufs=1))
+        arena = ctx.enter_context(tc.tile_pool(name="arena", bufs=1))
         keep = ctx.enter_context(tc.tile_pool(name="keep", bufs=1))
         stage = ctx.enter_context(tc.tile_pool(name="stage", bufs=2))
-        exps = ctx.enter_context(tc.tile_pool(name="exps", bufs=5))
-        banks = ctx.enter_context(tc.psum_pool(name="banks", bufs=8))
+        banks = ctx.enter_context(tc.psum_pool(name="banks", bufs=4))
 
         def held(name, shape, dtype):
             return keep.tile(shape, dtype, name=name, align_bytes=64)
 
-        pick = lists.tile([P, S // 16], U16, name="pick")
-        place = lists.tile([P, S // 16], U16, name="place")
-
-        tscale = held("tscale", [P, T], U8)
-        wbs_raw = held("wbs_raw", [P, PASSES * H], U8)
-        vplanes = held("vplanes", [P, PASSES * S], U8)
-        nc.gpsimd.memset(tscale[:].bitcast(I32), 0)
-        nc.gpsimd.memset(wbs_raw[:].bitcast(I32), 0)
-        nc.gpsimd.memset(vplanes[:].bitcast(I32), 0)
-
         def reused(name, tag, shape, dtype):
             return keep.tile(shape, dtype, name=name, tag=tag, align_bytes=64)
 
-        warm = held("warm", [P, 1], F32)
-        nc.vector.memset(warm[:], 0.0)
-        nc.scalar.activation(warm[:], warm[:], ACT.Exp)
+        def placed(name, offset, shape, dtype):
+            return arena.tile(shape, dtype, name=name, offset=offset, align_bytes=64)
+
+        pick = lists.tile([P, S // 16], U16, name="pick")
+        place = lists.tile([P, S // 16], U16, name="place")
+
+        tscale = placed("tscale", 0, [P, T], U8)
+        wbs_raw = held("wbs_raw", [P, H], U8)
+        nc.gpsimd.memset(tscale[:].bitcast(I32), 0)
+        nc.vector.memset(wbs_raw[:].bitcast(I32), 0)
         nc.sync.dma_start(pick[:], offs)
         nc.sync.dma_start(place[:], offs2)
         nc.sync.dma_start(
             out=tscale[0:P:4, :].bitcast(I32), in_=tab_scales.bitcast(I32).rearrange("a q t -> q a t")
         )
-        wa_raw = {}
+        nc.sync.dma_start(
+            out=wbs_raw[0:P:4, :].bitcast(I32), in_=wb_scales.bitcast(I32).rearrange("a q c -> q a c")
+        )
+        twords = [placed("twords0", 8256, [P, T], U32), reused("twords1", "tab1", [P, T], U32)]
 
-        def load_wa(a, b):
-            wa_raw[a, b] = reused(f"wa_raw{a}{b}", f"wa{a}", [P, 4, 512], F32)
-            nc.sync.dma_start(
-                out=wa_raw[a, b][:],
-                in_=wa[512 * a : 512 * (a + 1), 512 * b : 512 * (b + 1)].rearrange("(p i) c -> p i c", i=4),
-            )
-
-        twords = [reused(f"twords{a}", f"tab{a}", [P, T], U32) for a in range(PASSES)]
-
-        def load_twords(a):
+        def load_table(a):
             nc.sync.dma_start(
                 out=twords[a][:].bitcast(I32),
                 in_=tab_words[a].rearrange("p t i -> p (t i)").bitcast(I32),
             )
 
-        load_wa(0, 0)
-        wbs_rows = wb_scales.rearrange("a (d r) c -> r d a c", r=4)
-        for r in range(4):
-            nc.sync.dma_start(
-                out=wbs_raw[r:P:32, :].bitcast(I32).rearrange("d (a c) -> d a c", a=PASSES),
-                in_=wbs_rows[r].bitcast(I32),
-            )
-        load_twords(0)
-        load_wa(1, 0)
-        wbw_raw = reused("wbw_raw", "wb_in", [P, PASSES, H // 2], I32)
-        nc.sync.dma_start(out=wbw_raw[:], in_=wb_words.bitcast(I32).rearrange("a p c -> p a c"))
-        load_twords(1)
+        load_table(0)
+        wbw_raw = reused("wbw_raw", "wb", [P, PASSES * H // 2], I32)
+        nc.sync.dma_start(
+            out=wbw_raw[:].rearrange("p (a c) -> p a c", a=PASSES),
+            in_=wb_words.bitcast(I32).rearrange("a p c -> p a c"),
+        )
+        load_table(1)
 
-        gain_span = held("gain_span", [P, PASSES, 13], F32)
-        gain_rows = gain.rearrange("(b m x) -> m b x", b=PASSES, x=16)
-        for u in range(4):
-            nc.gpsimd.dma_start(out=gain_span[u:P:4, :, :], in_=gain_rows[:, :, u : u + 13])
-        gains = held("gains", [P, PASSES, 4], F32)
-        nc.gpsimd.tensor_copy(gains[:], gain_span[:, :, 0:13:4])
+        planes = held("planes", [P, PASSES, S + H], U8)
+        nc.vector.memset(planes[:].rearrange("p a c -> p (a c)").bitcast(I32), 0)
+        pages = {}
 
+        def clear(i, tile):
+            pages[i] = tile
+            for half in range(2):
+                nc.vector.memset(pages[i][:, 1024 * half : 1024 * (half + 1)].bitcast(I32), 0)
+
+        clear(0, held("page0", [P, T2], F32))
+
+        rows_in = reused("rows_in", "small", [P, S + H], U8)
+        nc.vector.tensor_copy(
+            rows_in[:, S:].bitcast(I32).rearrange("p (t m) -> p t m", t=4),
+            wbs_raw[:].bitcast(I32).rearrange("p (m t) -> p t m", t=4),
+        )
         gscale = held("gscale", [P, S], U8)
         nc.vector.tensor_copy(gscale[:], tscale[:].indirect(pick[:]))
+        nc.vector.tensor_copy(rows_in[:, 0:S].bitcast(I32), gscale[:].bitcast(I32))
         for d in range(4):
             nc.sync.dma_start(
-                out=vplanes[32 * d : 32 * d + 4, :].bitcast(I32),
-                in_=gscale[32 * d : 32 * (d + 1) : 4, :].bitcast(I32),
+                out=planes[32 * d : 32 * d + 4, :, :].rearrange("p a c -> p (a c)").bitcast(I32),
+                in_=rows_in[32 * d : 32 * (d + 1) : 4, :].bitcast(I32),
             )
+
+        wa_raw = {}
+
+        def load_wa(a, b, tile):
+            wa_raw[a, b] = tile
+            nc.sync.dma_start(
+                out=tile[:],
+                in_=wa[512 * a : 512 * (a + 1), 512 * b : 512 * (b + 1)].rearrange("(p i) c -> p i c", i=4),
+            )
+
+        load_wa(0, 0, placed("wa_raw00", 0, [P, 4, 512], F32))
+
         vwords = {}
-        for half in range(2):
-            for a in range(PASSES):
-                vwords[a, half] = held(f"vwords{a}{half}", [P, 512], U32)
-                nc.vector.tensor_copy(
-                    vwords[a, half][:], twords[a][:].indirect(pick[:, 32 * half : 32 * (half + 1)])
-                )
+
+        def gather(a, half):
+            vwords[a, half] = held(f"vwords{a}{half}", [P, HALF], U32)
+            nc.vector.tensor_copy(
+                vwords[a, half][:], twords[a][:].indirect(pick[:, 32 * half : 32 * (half + 1)])
+            )
 
         wbw = held("wbw", [P, PASSES * H // 2], I32)
-        nc.vector.tensor_copy(
-            wbw[:].rearrange("p (a t m u) -> p a t m u", a=PASSES, t=4, u=2),
-            wbw_raw[:].rearrange("p a (m t u) -> p a t m u", t=4, u=2),
-        )
-        wbs = held("wbs", [P, PASSES * H], U8)
-        nc.vector.tensor_copy(
-            wbs[:].bitcast(I32).rearrange("p (a t m) -> p a t m", a=PASSES, t=4),
-            wbs_raw[:].bitcast(I32).rearrange("p (a m t) -> p a t m", a=PASSES, t=4),
-        )
         wbw_bytes = wbw[:].bitcast(U8)
 
-        wa_q, wa_s = {}, {}
+        def order_wb():
+            nc.vector.tensor_copy(
+                wbw[:].rearrange("p (a t m u) -> p a t m u", a=PASSES, t=4, u=2),
+                wbw_raw[:].rearrange("p (a m t u) -> p a t m u", a=PASSES, t=4, u=2),
+            )
 
-        def prep_wa(a, b):
-            rounded = stage.tile([P, 2048], BF16, name="wa_bf", align_bytes=64)
-            (nc.scalar.copy if b == 0 else nc.vector.tensor_copy)(
-                rounded[:].rearrange("p (t m u i) -> p t m i u", t=4, u=4, i=4),
+        gains = held("gains", [P, PASSES, 4], F32)
+
+        def load_gains():
+            gain_span = reused("gain_span", "small", [P, PASSES, 13], F32)
+            gain_rows = gain.rearrange("(b m x) -> m b x", b=PASSES, x=16)
+            for u in range(4):
+                nc.sync.dma_start(out=gain_span[u:P:4, :, :], in_=gain_rows[:, :, u : u + 13])
+            nc.vector.tensor_copy(gains[:], gain_span[:, :, 0:13:4])
+
+        wa_bf, wa_q, wa_s = {}, {}, {}
+
+        def round_wa(a, b, copy):
+            if (a, b) == (1, 0):
+                wa_bf[a, b] = placed("wa_bf10", 30720, [P, 2048], BF16)
+            else:
+                wa_bf[a, b] = stage.tile([P, 2048], BF16, name="wa_bf", align_bytes=64)
+            copy(
+                wa_bf[a, b][:].rearrange("p (t m u i) -> p t m i u", t=4, u=4, i=4),
                 wa_raw[a, b][:].rearrange("p i (m t u) -> p t m i u", t=4, u=4),
             )
+
+        def quantise_wa(a, b):
             wa_q[a, b] = held(f"wa_q{a}{b}", [P, 512], U32)
             wa_s[a, b] = held(f"wa_s{a}{b}", [P, 512], U8)
-            nc.vector.quantize_mx(out=wa_q[a, b][:].bitcast(E4M3), scales=wa_s[a, b][:], in_=rounded[:])
+            nc.vector.quantize_mx(out=wa_q[a, b][:].bitcast(E4M3), scales=wa_s[a, b][:], in_=wa_bf[a, b][:])
 
-        wc_q, wc_s = {}, {}
+        wc_raw = {}
 
-        def prep_wc(b):
-            rounded = reused(f"wc_bf{b}", f"then{b + 2}", [P, 2048], BF16)
-            nc.scalar.copy(
-                rounded[:].rearrange("p (i q t) -> p q t i", i=4, t=4),
-                wc_raw[b][:].rearrange("p t (q i) -> p q t i", i=4),
+        def load_wc(b, tile):
+            wc_raw[b] = tile
+            rows = wc[512 * b : 512 * (b + 1), :].rearrange("(m t u) n -> t m u n", t=4, u=4)
+            for t in range(4):
+                nc.sync.dma_start(out=tile[:, t, :], in_=rows[t])
+
+        wc_bf, wc_q, wc_s = {}, {}, {}
+
+        def round_wc(pair):
+            wc_bf[pair] = stage.tile([P, PASSES, 1024], BF16, name="wc_bf", align_bytes=64)
+            for b in range(PASSES):
+                nc.scalar.copy(
+                    wc_bf[pair][:, b, :].rearrange("p (e q t) -> p q t e", e=2, t=4),
+                    wc_raw[b][:].rearrange("p t (q i) -> p q t i", i=4)[:, :, :, 2 * pair : 2 * pair + 2],
+                )
+
+        def quantise_wc(pair):
+            wc_q[pair] = held(f"wc_q{pair}", [P, 512], U32)
+            wc_s[pair] = held(f"wc_s{pair}", [P, 512], U8)
+            nc.vector.quantize_mx(
+                out=wc_q[pair][:].bitcast(E4M3),
+                scales=wc_s[pair][:],
+                in_=wc_bf[pair][:].rearrange("p b c -> p (b c)"),
             )
-            wc_q[b] = held(f"wc_q{b}", [P, N], U32)
-            wc_s[b] = held(f"wc_s{b}", [P, N], U8)
-            nc.vector.quantize_mx(out=wc_q[b][:].bitcast(E4M3), scales=wc_s[b][:], in_=rounded[:])
 
         ea, eb, hb, h_q, h_s = {}, {}, {}, {}, {}
 
-        def readings(b, g):
-            if b == 0 and g > 0:
-                ea[b, g] = reused(f"ea0{g}", f"then{g}", [P, 4 * GRP], F32)
-            else:
-                ea[b, g] = exps.tile([P, 4 * GRP], F32, name="ea", align_bytes=64)
-            eb[b, g] = exps.tile([P, 4 * GRP], F32, name="eb", align_bytes=64)
-            for s in range(GRP // BLK):
-                j0 = g * GRP + s * BLK
-                half, c0 = divmod(j0, 512)
-                bank_a = banks.tile([P, 4, BLK], F32, name="bank_a", tag="bank")
-                bank_b = banks.tile([P, 4, BLK], F32, name="bank_b", tag="bank")
-                for t in range(4):
-                    for a in range(PASSES):
-                        nc.tensor.matmul_mx(
-                            out=bank_a[:, t, :],
-                            lhsT=wa_q[a, b][:, P * t : P * (t + 1)].bitcast(E4M3),
-                            lhsT_scale=wa_s[a, b][:, P * t : P * (t + 1)],
-                            rhs=vwords[a, half][:, c0 : c0 + BLK].bitcast(E4M3),
-                            rhs_scale=vplanes[:, a * S + j0 : a * S + j0 + BLK],
-                            start=(a == 0),
-                            stop=(a == PASSES - 1),
-                        )
-                nc.scalar.activation(
-                    ea[b, g][:, 4 * BLK * s : 4 * BLK * (s + 1)].rearrange("p (j t) -> p j t", t=4),
-                    bank_a[:].rearrange("p t j -> p j t"),
-                    ACT.Exp,
+        def read_a(b, half, t):
+            if t == 0:
+                ea[b, half] = held(f"ea{b}{half}", [P, 4, HALF], F32)
+            bank = banks.tile([P, HALF], F32, name="bank_a", tag="for_a")
+            for a in range(PASSES):
+                nc.tensor.matmul_mx(
+                    out=bank[:],
+                    lhsT=wa_q[a, b][:, P * t : P * (t + 1)].bitcast(E4M3),
+                    lhsT_scale=wa_s[a, b][:, P * t : P * (t + 1)],
+                    rhs=vwords[a, half][:].bitcast(E4M3),
+                    rhs_scale=planes[:, a, half * HALF : (half + 1) * HALF],
+                    start=(a == 0),
+                    stop=(a == PASSES - 1),
                 )
-                for t in range(4):
-                    for a in range(PASSES):
-                        col = a * H + t * 256 + b * P
-                        nc.tensor.matmul_mx(
-                            out=bank_b[:, t, :],
-                            lhsT=wbw_bytes[:, 2 * col : 2 * (col + P)].bitcast(E2M1),
-                            lhsT_scale=wbs[:, col : col + P],
-                            rhs=vwords[a, half][:, c0 : c0 + BLK].bitcast(E4M3),
-                            rhs_scale=vplanes[:, a * S + j0 : a * S + j0 + BLK],
-                            start=(a == 0),
-                            stop=(a == PASSES - 1),
-                        )
-                nc.scalar.activation(
-                    eb[b, g][:, 4 * BLK * s : 4 * BLK * (s + 1)].rearrange("p (j t) -> p j t", t=4),
-                    bank_b[:].rearrange("p t j -> p j t"),
-                    ACT.Exp,
+            nc.scalar.activation(ea[b, half][:, t, :], bank[:], ACT.Exp)
+
+        def read_b(b, half, t):
+            if t == 0:
+                eb[b, half] = reused(f"eb{b}{half}", f"eb{half}", [P, 4, HALF], F32)
+            bank = banks.tile([P, HALF], F32, name="bank_b", tag="for_b")
+            col = t * 256 + b * P
+            for a in range(PASSES):
+                nc.tensor.matmul_mx(
+                    out=bank[:],
+                    lhsT=wbw_bytes[:, 2 * (a * H + col) : 2 * (a * H + col + P)].bitcast(E2M1),
+                    lhsT_scale=planes[:, a, S + col : S + col + P],
+                    rhs=vwords[a, half][:].bitcast(E4M3),
+                    rhs_scale=planes[:, a, half * HALF : (half + 1) * HALF],
+                    start=(a == 0),
+                    stop=(a == PASSES - 1),
                 )
+            nc.scalar.activation(eb[b, half][:, t, :], bank[:], ACT.Exp)
 
-        diff = {}
+        def read(b, half, *readings):
+            for t in range(4):
+                for reading in readings:
+                    reading(b, half, t)
 
-        def subtract(b, g):
-            diff[b, g] = stage.tile([P, 4 * GRP], F32, name="diff", align_bytes=64)
-            nc.vector.tensor_tensor(diff[b, g][:], ea[b, g][:], eb[b, g][:], ALU.subtract)
-
-        def scale(b, g):
-            hb[b, g] = stage.tile([P, 4 * GRP], BF16, name="hb", align_bytes=64)
+        def subtract(b, half, pair):
+            codes = slice(2 * pair, 2 * pair + 2)
             nc.vector.tensor_tensor(
-                hb[b, g][:].rearrange("p (j t) -> p j t", t=4),
-                diff[b, g][:].rearrange("p (j t) -> p j t", t=4),
-                gains[:, b, :].unsqueeze(1).to_broadcast([P, GRP, 4]),
+                ea[b, half][:, codes, :], ea[b, half][:, codes, :], eb[b, half][:, codes, :], ALU.subtract
+            )
+
+        def scale(b, half, part):
+            if part == 0:
+                hb[b, half] = stage.tile([P, 4 * HALF], BF16, name="hb", align_bytes=64)
+            nc.vector.tensor_tensor(
+                hb[b, half][:, 4 * QUART * part : 4 * QUART * (part + 1)].rearrange(
+                    "p (c i t) -> p c t i", i=4, t=4
+                ),
+                ea[b, half][:, :, QUART * part : QUART * (part + 1)].rearrange("p t (c i) -> p c t i", i=4),
+                gains[:, b, :].unsqueeze(1).unsqueeze(3).to_broadcast([P, QUART // 4, 4, 4]),
                 ALU.mult,
             )
 
-        def quantise(b, g):
-            h_q[b, g] = held(f"h_q{b}{g}", [P, GRP], U32)
-            h_s[b, g] = held(f"h_s{b}{g}", [P, GRP], U8)
-            nc.vector.quantize_mx(out=h_q[b, g][:].bitcast(E4M3), scales=h_s[b, g][:], in_=hb[b, g][:])
+        def quantise_h(b, half):
+            h_q[b, half] = held(f"h_q{b}{half}", [P, HALF], U32)
+            h_s[b, half] = held(f"h_s{b}{half}", [P, HALF], U8)
+            nc.vector.quantize_mx(out=h_q[b, half][:].bitcast(E4M3), scales=h_s[b, half][:], in_=hb[b, half][:])
 
-        chunks = ((0,), (1,), (2, 3))
-        ys = [held(f"y{c}", [P, 4, GRP * len(gs)], F32) for c, gs in enumerate(chunks)]
+        def cues(b, half, between, later=lambda: None):
+            subtract(b, half, 0)
+            subtract(b, half, 1)
+            between()
+            scale(b, half, 0)
+            later()
+            scale(b, half, 1)
 
-        def mix(g, pair, y, at):
-            if True:
-                bank = banks.tile([P, 2, GRP], F32, name="bank_c", tag="bank")
-                for e in range(2):
-                    i = 2 * pair + e
-                    for b in range(PASSES):
-                        nc.tensor.matmul_mx(
-                            out=bank[:, e, :],
-                            lhsT=wc_q[b][:, P * i : P * (i + 1)].bitcast(E4M3),
-                            lhsT_scale=wc_s[b][:, P * i : P * (i + 1)],
-                            rhs=h_q[b, g][:].bitcast(E4M3),
-                            rhs_scale=h_s[b, g][:],
-                            start=(b == 0),
-                            stop=(b == PASSES - 1),
-                        )
-                dst = y[:, 2 * pair : 2 * pair + 2, at * GRP : (at + 1) * GRP]
-                nc.scalar.activation(dst, bank[:], ACT.Square)
+        gather(0, 0)
+        gather(0, 1)
+        load_wa(1, 0, placed("wa_raw10", 8256, [P, 4, 512], F32))
+        order_wb()
+        load_wa(0, 1, reused("wa_raw01", "wb", [P, 4, 512], F32))
+        gather(1, 0)
+        read(0, 0, read_b)
+        gather(1, 1)
+        load_wa(1, 1, reused("wa_raw11", "tab1", [P, 4, 512], F32))
+        read(0, 1, read_b)
+        load_gains()
+        round_wa(0, 0, nc.vector.tensor_copy)
+        load_wc(0, placed("wc_raw0", 0, [P, 4, N], F32))
+        quantise_wa(0, 0)
+        round_wa(1, 0, nc.vector.tensor_copy)
+        load_wc(1, placed("wc_raw1", 8192, [P, 4, N], F32))
+        quantise_wa(1, 0)
+        clear(3, placed("page3", 16384, [P, T2], F32))
+        clear(1, placed("page1", 24576, [P, T2], F32))
+        clear(2, placed("page2", 32768, [P, T2], F32))
+        read(0, 0, read_a)
+        read(0, 1, read_a)
+        round_wa(0, 1, nc.scalar.copy)
+        weights = reused("weights", "wb", [P, S], F32)
+        nc.sync.dma_start(out=weights[:], in_=wgo)
+        round_wa(1, 1, nc.scalar.copy)
+        cues(0, 0, lambda: quantise_wa(0, 1))
+        cues(0, 1, lambda: quantise_h(0, 0), lambda: quantise_wa(1, 1))
+        read(1, 0, read_b)
+        read(1, 0, read_a)
+        round_wc(0)
+        read(1, 1, read_b, read_a)
+        cues(1, 0, lambda: quantise_h(0, 1))
+        quantise_wc(0)
+        cues(1, 1, lambda: quantise_h(1, 0))
+        quantise_h(1, 1)
 
-        units = [(b, g) for b in range(PASSES) for g in range(GROUPS)]
-        prep_wa(0, 0)
-        prep_wa(1, 0)
-        load_wa(0, 1)
-        load_wa(1, 1)
-        wc_raw = {}
+        ys = [held(f"y{pair}", [P, 2, S], F32) for pair in range(2)]
 
-        def load_wc(b):
-            wc_raw[b] = reused(f"wc_raw{b}", f"wa{b}", [P, 4, N], F32)
-            rows = wc[512 * b : 512 * (b + 1), :].rearrange("(m t u) n -> t m u n", t=4, u=4)
-            for t in range(4):
-                nc.sync.dma_start(out=wc_raw[b][:, t, :], in_=rows[t])
-
-        for k in range(len(units) + 2):
-            if k in (0, 1):
-                prep_wa(k, 1)
-                load_wc(k)
-            if k < len(units):
-                readings(*units[k])
-                subtract(*units[k])
-            if k == 1:
-                weights = reused("weights", "then1", [P, S], F32)
-                nc.sync.dma_start(out=weights[:], in_=wgo)
-            if k in (4, 5):
-                prep_wc(k - 4)
-            if 1 <= k <= len(units):
-                scale(*units[k - 1])
-            if k >= 2:
-                quantise(*units[k - 2])
-
-        pages = [held(f"page{i}", [P, T2], F32) for i in range(4)]
-        for i in range(2):
-            for half in range(2):
-                nc.vector.memset(pages[i][:, 1024 * half : 1024 * (half + 1)], 0.0)
-        for i in range(2, 4):
-            for part in range(4):
-                nc.gpsimd.memset(pages[i][:, 512 * part : 512 * (part + 1)], 0.0)
-
-        for gs, y in zip(chunks, ys):
-            for pair in range(2):
-                for at, g in enumerate(gs):
-                    mix(g, pair, y, at)
-                both = y[:, 2 * pair : 2 * pair + 2, :]
-                nc.scalar.activation(both, both, ACT.Ln, bias=1.0)
-        rows = out.rearrange("(p i) t -> i p t", i=4)
-        for gs, y in zip(chunks, ys):
-            j0, j1 = GRP * gs[0], GRP * (gs[-1] + 1)
-            for i in range(4):
-                nc.vector.tensor_tensor(
-                    pages[i][:].indirect(place[:, j0 // 16 : j1 // 16]), y[:, i, :], weights[:, j0:j1], ALU.mult
+        def mix(i, half):
+            pair, e = divmod(i, 2)
+            bank = banks.tile([P, HALF], F32, name="bank_c", tag="for_a")
+            for b in range(PASSES):
+                col = 256 * b + P * e
+                nc.tensor.matmul_mx(
+                    out=bank[:],
+                    lhsT=wc_q[pair][:, col : col + P].bitcast(E4M3),
+                    lhsT_scale=wc_s[pair][:, col : col + P],
+                    rhs=h_q[b, half][:].bitcast(E4M3),
+                    rhs_scale=h_s[b, half][:],
+                    start=(b == 0),
+                    stop=(b == PASSES - 1),
                 )
-                if j1 == S:
-                    nc.sync.dma_start(out=rows[i], in_=pages[i][:])
+            y = ys[pair][:, e, HALF * half : HALF * (half + 1)]
+            nc.scalar.activation(y, bank[:], ACT.Square)
+            nc.scalar.activation(y, y, ACT.Ln, bias=1.0)
+
+        rows = out.rearrange("(p i) t -> i p t", i=4)
+
+        def scatter(i, j0, j1):
+            pair, e = divmod(i, 2)
+            nc.vector.tensor_tensor(
+                pages[i][:].indirect(place[:, j0 // 16 : j1 // 16]),
+                ys[pair][:, e, j0:j1],
+                weights[:, j0:j1],
+                ALU.mult,
+            )
+            if j1 == S:
+                nc.sync.dma_start(out=rows[i], in_=pages[i][:])
+
+        for half in range(2):
+            for i in range(2):
+                mix(i, half)
+        round_wc(1)
+        for half in range(2):
+            for i in range(2):
+                scatter(i, HALF * half, HALF * (half + 1))
+        quantise_wc(1)
+        for i in range(2, 4):
+            for half in range(2):
+                mix(i, half)
+            scatter(i, 0, S)

@@ -162,10 +162,10 @@ def tile_list_baggage_density_cues_kernel(
 
         wc_bf, wc_q, wc_s = {}, {}, {}
 
-        def round_wc(pair):
+        def round_wc(pair, copy):
             wc_bf[pair] = stage.tile([P, PASSES, 1024], BF16, name="wc_bf", align_bytes=64)
             for b in range(PASSES):
-                nc.scalar.copy(
+                copy(
                     wc_bf[pair][:, b, :].rearrange("p (e q t) -> p q t e", e=2, t=4),
                     wc_raw[b][:].rearrange("p t (q i) -> p q t i", i=4)[:, :, :, 2 * pair : 2 * pair + 2],
                 )
@@ -272,18 +272,18 @@ def tile_list_baggage_density_cues_kernel(
         clear(2, placed("page2", 32768, [P, T2], F32))
         read(0, 0, read_a)
         read(0, 1, read_a)
-        round_wa(0, 1, nc.scalar.copy)
+        round_wa(0, 1, nc.vector.tensor_copy)
         weights = reused("weights", "wb", [P, S], F32)
         nc.sync.dma_start(out=weights[:], in_=wgo)
-        round_wa(1, 1, nc.scalar.copy)
-        cues(0, 0, lambda: quantise_wa(0, 1))
-        cues(0, 1, lambda: quantise_h(0, 0), lambda: quantise_wa(1, 1))
+        round_wa(1, 1, nc.vector.tensor_copy)
+        quantise_wa(0, 1)
+        cues(0, 0, lambda: quantise_wa(1, 1))
+        cues(0, 1, lambda: quantise_h(0, 0))
+        round_wc(0, nc.vector.tensor_copy)
         read(1, 0, read_b)
         read(1, 0, read_a)
-        round_wc(0)
         read(1, 1, read_b, read_a)
-        cues(1, 0, lambda: quantise_h(0, 1))
-        quantise_wc(0)
+        cues(1, 0, lambda: quantise_h(0, 1), lambda: quantise_wc(0))
         cues(1, 1, lambda: quantise_h(1, 0))
         quantise_h(1, 1)
 
@@ -323,7 +323,7 @@ def tile_list_baggage_density_cues_kernel(
         for half in range(2):
             for i in range(2):
                 mix(i, half)
-        round_wc(1)
+        round_wc(1, nc.scalar.copy)
         for half in range(2):
             for i in range(2):
                 scatter(i, HALF * half, HALF * (half + 1))

@@ -1,6 +1,7 @@
 from contextlib import ExitStack
 
 import concourse.mybir as mybir
+from concourse.masks import make_identity
 
 K, H, N, T, S, T2 = 1024, 1024, 512, 2048, 1024, 2048
 FLOPS = 2 * (2 * K * H * S + H * N * S)
@@ -20,6 +21,8 @@ P = 128
 PASSES = 2
 HALF = S // 2
 QUART = S // 4
+WA_BF_AT = {(0, 0): 65536, (1, 0): 40960, (0, 1): 57344, (1, 1): 24576}
+EB_AT = {(0, 0): 69632, (0, 1): 40960, (1, 0): 57344, (1, 1): 69632}
 
 
 def tile_list_baggage_density_cues_kernel(
@@ -31,7 +34,13 @@ def tile_list_baggage_density_cues_kernel(
         arena = ctx.enter_context(tc.tile_pool(name="arena", bufs=1))
         keep = ctx.enter_context(tc.tile_pool(name="keep", bufs=1))
         stage = ctx.enter_context(tc.tile_pool(name="stage", bufs=2))
-        banks = ctx.enter_context(tc.psum_pool(name="banks", bufs=4))
+        banks = ctx.enter_context(tc.psum_pool(name="banks", bufs=1))
+        taken = []
+
+        def next_bank():
+            k = len(taken)
+            taken.append(k)
+            return banks.tile([P, HALF], F32, name=f"bank{k}", offset=2048 * (k % 7))
 
         def held(name, shape, dtype):
             return keep.tile(shape, dtype, name=name, align_bytes=64)
@@ -57,7 +66,7 @@ def tile_list_baggage_density_cues_kernel(
         nc.sync.dma_start(
             out=wbs_raw[0:P:4, :].bitcast(I32), in_=wb_scales.bitcast(I32).rearrange("a q c -> q a c")
         )
-        twords = [placed("twords0", 8256, [P, T], U32), reused("twords1", "tab1", [P, T], U32)]
+        twords = [placed("twords0", 8192, [P, T], U32), reused("twords1", "tab1", [P, T], U32)]
 
         def load_table(a):
             nc.sync.dma_start(
@@ -77,12 +86,9 @@ def tile_list_baggage_density_cues_kernel(
         nc.vector.memset(planes[:].rearrange("p a c -> p (a c)").bitcast(I32), 0)
         pages = {}
 
-        def clear(i, tile):
-            pages[i] = tile
-            for half in range(2):
-                nc.vector.memset(pages[i][:, 1024 * half : 1024 * (half + 1)].bitcast(I32), 0)
-
-        clear(0, held("page0", [P, T2], F32))
+        def clear_beside(i, offset):
+            pages[i] = placed(f"page{i}", offset, [P, T2], F32)
+            nc.gpsimd.memset(pages[i][:].bitcast(I32), 0)
 
         rows_in = reused("rows_in", "small", [P, S + H], U8)
         nc.vector.tensor_copy(
@@ -126,22 +132,24 @@ def tile_list_baggage_density_cues_kernel(
                 wbw_raw[:].rearrange("p (a m t u) -> p a t m u", a=PASSES, t=4, u=2),
             )
 
-        gains = held("gains", [P, PASSES, 4], F32)
+        gains = banks.tile([P, PASSES, P], F32, name="gains", offset=2048 * 7)
 
         def load_gains():
-            gain_span = reused("gain_span", "small", [P, PASSES, 13], F32)
-            gain_rows = gain.rearrange("(b m x) -> m b x", b=PASSES, x=16)
-            for u in range(4):
-                nc.sync.dma_start(out=gain_span[u:P:4, :, :], in_=gain_rows[:, :, u : u + 13])
-            nc.vector.tensor_copy(gains[:], gain_span[:, :, 0:13:4])
+            identity = held("identity", [P, P], F32)
+            make_identity(nc, identity[:])
+            gain_rows = held("gain_rows", [P, PASSES * P], F32)
+            nc.gpsimd.memset(gain_rows[:], 0.0)
+            nc.sync.dma_start(
+                out=gain_rows[0:4, :].rearrange("t (m u) -> t m u", u=4),
+                in_=gain.rearrange("(m t u) -> t m u", t=4, u=4),
+            )
+            for b in range(PASSES):
+                nc.tensor.transpose(gains[:, b, :], gain_rows[:, P * b : P * (b + 1)], identity[:])
 
         wa_bf, wa_q, wa_s = {}, {}, {}
 
         def round_wa(a, b, copy):
-            if (a, b) == (1, 0):
-                wa_bf[a, b] = placed("wa_bf10", 30720, [P, 2048], BF16)
-            else:
-                wa_bf[a, b] = stage.tile([P, 2048], BF16, name="wa_bf", align_bytes=64)
+            wa_bf[a, b] = placed(f"wa_bf{a}{b}", WA_BF_AT[a, b], [P, 2048], BF16)
             copy(
                 wa_bf[a, b][:].rearrange("p (t m u i) -> p t m i u", t=4, u=4, i=4),
                 wa_raw[a, b][:].rearrange("p i (m t u) -> p t m i u", t=4, u=4),
@@ -162,12 +170,12 @@ def tile_list_baggage_density_cues_kernel(
 
         wc_bf, wc_q, wc_s = {}, {}, {}
 
-        def round_wc(pair, copy):
+        def round_wc(pair):
             wc_bf[pair] = stage.tile([P, PASSES, 1024], BF16, name="wc_bf", align_bytes=64)
             for b in range(PASSES):
-                copy(
-                    wc_bf[pair][:, b, :].rearrange("p (e q t) -> p q t e", e=2, t=4),
-                    wc_raw[b][:].rearrange("p t (q i) -> p q t i", i=4)[:, :, :, 2 * pair : 2 * pair + 2],
+                nc.scalar.copy(
+                    wc_bf[pair][:, b, :].rearrange("p (e q t) -> p q e t", e=2, t=4),
+                    wc_raw[b][:].rearrange("p t (q i) -> p q i t", i=4)[:, :, 2 * pair : 2 * pair + 2, :],
                 )
 
         def quantise_wc(pair):
@@ -184,7 +192,7 @@ def tile_list_baggage_density_cues_kernel(
         def read_a(b, half, t):
             if t == 0:
                 ea[b, half] = held(f"ea{b}{half}", [P, 4, HALF], F32)
-            bank = banks.tile([P, HALF], F32, name="bank_a", tag="for_a")
+            bank = next_bank()
             for a in range(PASSES):
                 nc.tensor.matmul_mx(
                     out=bank[:],
@@ -199,8 +207,8 @@ def tile_list_baggage_density_cues_kernel(
 
         def read_b(b, half, t):
             if t == 0:
-                eb[b, half] = reused(f"eb{b}{half}", f"eb{half}", [P, 4, HALF], F32)
-            bank = banks.tile([P, HALF], F32, name="bank_b", tag="for_b")
+                eb[b, half] = placed(f"eb{b}{half}", EB_AT[b, half], [P, 4, HALF], F32)
+            bank = next_bank()
             col = t * 256 + b * P
             for a in range(PASSES):
                 nc.tensor.matmul_mx(
@@ -219,47 +227,56 @@ def tile_list_baggage_density_cues_kernel(
                 for reading in readings:
                     reading(b, half, t)
 
-        def subtract(b, half, pair):
-            codes = slice(2 * pair, 2 * pair + 2)
-            nc.vector.tensor_tensor(
-                ea[b, half][:, codes, :], ea[b, half][:, codes, :], eb[b, half][:, codes, :], ALU.subtract
-            )
+        def subtract(b, half, part):
+            if (b, half) == (0, 0):
+                where = (slice(None), slice(2 * part, 2 * part + 2), slice(None))
+            else:
+                where = (slice(None), slice(None), slice(QUART * part, QUART * (part + 1)))
+            nc.vector.tensor_tensor(ea[b, half][where], ea[b, half][where], eb[b, half][where], ALU.subtract)
 
         def scale(b, half, part):
             if part == 0:
-                hb[b, half] = stage.tile([P, 4 * HALF], BF16, name="hb", align_bytes=64)
+                if (b, half) == (1, 1):
+                    hb[b, half] = held("hb11", [P, 4 * HALF], BF16)
+                else:
+                    hb[b, half] = placed(f"hb{b}{half}", (32768, 16384, 49152)[2 * b + half], [P, 4 * HALF], BF16)
             nc.vector.tensor_tensor(
                 hb[b, half][:, 4 * QUART * part : 4 * QUART * (part + 1)].rearrange(
                     "p (c i t) -> p c t i", i=4, t=4
                 ),
                 ea[b, half][:, :, QUART * part : QUART * (part + 1)].rearrange("p t (c i) -> p c t i", i=4),
-                gains[:, b, :].unsqueeze(1).unsqueeze(3).to_broadcast([P, QUART // 4, 4, 4]),
+                gains[:, b, 0:4].unsqueeze(1).unsqueeze(3).to_broadcast([P, QUART // 4, 4, 4]),
                 ALU.mult,
             )
 
-        def quantise_h(b, half):
+        def quantise_h(b, half, parts=1):
             h_q[b, half] = held(f"h_q{b}{half}", [P, HALF], U32)
             h_s[b, half] = held(f"h_s{b}{half}", [P, HALF], U8)
-            nc.vector.quantize_mx(out=h_q[b, half][:].bitcast(E4M3), scales=h_s[b, half][:], in_=hb[b, half][:])
+            width = HALF // parts
+            for c0 in range(0, HALF, width):
+                nc.vector.quantize_mx(
+                    out=h_q[b, half][:, c0 : c0 + width].bitcast(E4M3),
+                    scales=h_s[b, half][:, c0 : c0 + width],
+                    in_=hb[b, half][:, 4 * c0 : 4 * (c0 + width)],
+                )
 
         def cues(b, half, between, later=lambda: None):
             subtract(b, half, 0)
-            subtract(b, half, 1)
             between()
-            scale(b, half, 0)
+            subtract(b, half, 1)
             later()
+            scale(b, half, 0)
             scale(b, half, 1)
 
         gather(0, 0)
         gather(0, 1)
-        load_wa(1, 0, placed("wa_raw10", 8256, [P, 4, 512], F32))
+        load_wa(1, 0, placed("wa_raw10", 8192, [P, 4, 512], F32))
         order_wb()
         load_wa(0, 1, reused("wa_raw01", "wb", [P, 4, 512], F32))
         gather(1, 0)
         read(0, 0, read_b)
         gather(1, 1)
         load_wa(1, 1, reused("wa_raw11", "tab1", [P, 4, 512], F32))
-        read(0, 1, read_b)
         load_gains()
         round_wa(0, 0, nc.vector.tensor_copy)
         load_wc(0, placed("wc_raw0", 0, [P, 4, N], F32))
@@ -267,31 +284,34 @@ def tile_list_baggage_density_cues_kernel(
         round_wa(1, 0, nc.vector.tensor_copy)
         load_wc(1, placed("wc_raw1", 8192, [P, 4, N], F32))
         quantise_wa(1, 0)
-        clear(3, placed("page3", 16384, [P, T2], F32))
-        clear(1, placed("page1", 24576, [P, T2], F32))
-        clear(2, placed("page2", 32768, [P, T2], F32))
         read(0, 0, read_a)
+        read(0, 1, read_b)
         read(0, 1, read_a)
         round_wa(0, 1, nc.vector.tensor_copy)
         weights = reused("weights", "wb", [P, S], F32)
         nc.sync.dma_start(out=weights[:], in_=wgo)
-        round_wa(1, 1, nc.vector.tensor_copy)
         quantise_wa(0, 1)
-        cues(0, 0, lambda: quantise_wa(1, 1))
-        cues(0, 1, lambda: quantise_h(0, 0))
-        round_wc(0, nc.vector.tensor_copy)
+        cues(0, 0, lambda: round_wa(1, 1, nc.vector.tensor_copy), lambda: quantise_wa(1, 1))
+        clear_beside(0, 24576)
         read(1, 0, read_b)
         read(1, 0, read_a)
+        round_wc(0)
         read(1, 1, read_b, read_a)
-        cues(1, 0, lambda: quantise_h(0, 1), lambda: quantise_wc(0))
-        cues(1, 1, lambda: quantise_h(1, 0))
-        quantise_h(1, 1)
+        cues(0, 1, lambda: quantise_h(0, 0))
+        clear_beside(1, 32768)
+        cues(1, 0, lambda: quantise_h(0, 1))
+        clear_beside(2, 16384)
+        quantise_wc(0)
+        quantise_h(1, 0, parts=2)
+        clear_beside(3, 49152)
+        cues(1, 1, lambda: None)
+        quantise_h(1, 1, parts=2)
 
         ys = [held(f"y{pair}", [P, 2, S], F32) for pair in range(2)]
 
         def mix(i, half):
             pair, e = divmod(i, 2)
-            bank = banks.tile([P, HALF], F32, name="bank_c", tag="for_a")
+            bank = next_bank()
             for b in range(PASSES):
                 col = 256 * b + P * e
                 nc.tensor.matmul_mx(
@@ -320,14 +340,15 @@ def tile_list_baggage_density_cues_kernel(
             if j1 == S:
                 nc.sync.dma_start(out=rows[i], in_=pages[i][:])
 
-        for half in range(2):
-            for i in range(2):
-                mix(i, half)
-        round_wc(1, nc.scalar.copy)
-        for half in range(2):
-            for i in range(2):
-                scatter(i, HALF * half, HALF * (half + 1))
+        for i in range(2):
+            mix(i, 0)
+        round_wc(1)
+        for i in range(2):
+            scatter(i, 0, HALF)
         quantise_wc(1)
+        for i in range(2):
+            mix(i, 1)
+            scatter(i, HALF, S)
         for i in range(2, 4):
             for half in range(2):
                 mix(i, half)

@@ -22,7 +22,7 @@ PASSES = 2
 HALF = S // 2
 QUART = S // 4
 WA_BF_AT = {(0, 0): 65536, (1, 0): 40960, (0, 1): 57344, (1, 1): 24576}
-EB_AT = {(0, 0): 69632, (0, 1): 40960, (1, 0): 57344, (1, 1): 69632}
+EB_AT = {(0, 0): 69632, (0, 1): 77824, (1, 0): 40960, (1, 1): 57344}
 
 
 def tile_list_baggage_density_cues_kernel(
@@ -33,7 +33,6 @@ def tile_list_baggage_density_cues_kernel(
         lists = ctx.enter_context(tc.tile_pool(name="lists", bufs=1))
         arena = ctx.enter_context(tc.tile_pool(name="arena", bufs=1))
         keep = ctx.enter_context(tc.tile_pool(name="keep", bufs=1))
-        stage = ctx.enter_context(tc.tile_pool(name="stage", bufs=2))
         banks = ctx.enter_context(tc.psum_pool(name="banks", bufs=1))
         taken = []
 
@@ -170,12 +169,12 @@ def tile_list_baggage_density_cues_kernel(
 
         wc_bf, wc_q, wc_s = {}, {}, {}
 
-        def round_wc(pair):
-            wc_bf[pair] = stage.tile([P, PASSES, 1024], BF16, name="wc_bf", align_bytes=64)
+        def round_wc(pair, copy):
+            wc_bf[pair] = placed(f"wc_bf{pair}", (90112, 86016)[pair], [P, PASSES, 1024], BF16)
             for b in range(PASSES):
-                nc.scalar.copy(
-                    wc_bf[pair][:, b, :].rearrange("p (e q t) -> p q e t", e=2, t=4),
-                    wc_raw[b][:].rearrange("p t (q i) -> p q i t", i=4)[:, :, 2 * pair : 2 * pair + 2, :],
+                copy(
+                    wc_bf[pair][:, b, :].rearrange("p (e q t) -> p q t e", e=2, t=4),
+                    wc_raw[b][:].rearrange("p t (q i) -> p q t i", i=4)[:, :, :, 2 * pair : 2 * pair + 2],
                 )
 
         def quantise_wc(pair):
@@ -222,13 +221,13 @@ def tile_list_baggage_density_cues_kernel(
                 )
             nc.scalar.activation(eb[b, half][:, t, :], bank[:], ACT.Exp)
 
-        def read(b, half, *readings):
-            for t in range(4):
+        def read(b, half, *readings, codes=range(4)):
+            for t in codes:
                 for reading in readings:
                     reading(b, half, t)
 
         def subtract(b, half, part):
-            if (b, half) == (0, 0):
+            if b == half:
                 where = (slice(None), slice(2 * part, 2 * part + 2), slice(None))
             else:
                 where = (slice(None), slice(None), slice(QUART * part, QUART * (part + 1)))
@@ -236,10 +235,7 @@ def tile_list_baggage_density_cues_kernel(
 
         def scale(b, half, part):
             if part == 0:
-                if (b, half) == (1, 1):
-                    hb[b, half] = held("hb11", [P, 4 * HALF], BF16)
-                else:
-                    hb[b, half] = placed(f"hb{b}{half}", (32768, 16384, 49152)[2 * b + half], [P, 4 * HALF], BF16)
+                hb[b, half] = placed(f"hb{b}{half}", (32768, 16384, 49152, 86016)[2 * b + half], [P, 4 * HALF], BF16)
             nc.vector.tensor_tensor(
                 hb[b, half][:, 4 * QUART * part : 4 * QUART * (part + 1)].rearrange(
                     "p (c i t) -> p c t i", i=4, t=4
@@ -277,6 +273,7 @@ def tile_list_baggage_density_cues_kernel(
         read(0, 0, read_b)
         gather(1, 1)
         load_wa(1, 1, reused("wa_raw11", "tab1", [P, 4, 512], F32))
+        read(0, 1, read_b, codes=range(2))
         load_gains()
         round_wa(0, 0, nc.vector.tensor_copy)
         load_wc(0, placed("wc_raw0", 0, [P, 4, N], F32))
@@ -285,7 +282,8 @@ def tile_list_baggage_density_cues_kernel(
         load_wc(1, placed("wc_raw1", 8192, [P, 4, N], F32))
         quantise_wa(1, 0)
         read(0, 0, read_a)
-        read(0, 1, read_b)
+        taken.extend(range(3))
+        read(0, 1, read_b, codes=range(2, 4))
         read(0, 1, read_a)
         round_wa(0, 1, nc.vector.tensor_copy)
         weights = reused("weights", "wb", [P, S], F32)
@@ -295,11 +293,10 @@ def tile_list_baggage_density_cues_kernel(
         clear_beside(0, 24576)
         read(1, 0, read_b)
         read(1, 0, read_a)
-        round_wc(0)
         read(1, 1, read_b, read_a)
         cues(0, 1, lambda: quantise_h(0, 0))
         clear_beside(1, 32768)
-        cues(1, 0, lambda: quantise_h(0, 1))
+        cues(1, 0, lambda: (round_wc(0, nc.vector.tensor_copy), quantise_h(0, 1)))
         clear_beside(2, 16384)
         quantise_wc(0)
         quantise_h(1, 0, parts=2)
@@ -342,7 +339,7 @@ def tile_list_baggage_density_cues_kernel(
 
         for i in range(2):
             mix(i, 0)
-        round_wc(1)
+        round_wc(1, nc.scalar.copy)
         for i in range(2):
             scatter(i, 0, HALF)
         quantise_wc(1)

@@ -169,12 +169,12 @@ def tile_list_baggage_density_cues_kernel(
 
         wc_bf, wc_q, wc_s = {}, {}, {}
 
-        def round_wc(pair, copy):
+        def round_wc(pair):
             wc_bf[pair] = placed(f"wc_bf{pair}", (90112, 86016)[pair], [P, PASSES, 1024], BF16)
             for b in range(PASSES):
-                copy(
-                    wc_bf[pair][:, b, :].rearrange("p (e q t) -> p q t e", e=2, t=4),
-                    wc_raw[b][:].rearrange("p t (q i) -> p q t i", i=4)[:, :, :, 2 * pair : 2 * pair + 2],
+                nc.scalar.copy(
+                    wc_bf[pair][:, b, :].rearrange("p (e q t) -> p q e t", e=2, t=4),
+                    wc_raw[b][:].rearrange("p t (q i) -> p q i t", i=4)[:, :, 2 * pair : 2 * pair + 2, :],
                 )
 
         def quantise_wc(pair):
@@ -293,10 +293,11 @@ def tile_list_baggage_density_cues_kernel(
         clear_beside(0, 24576)
         read(1, 0, read_b)
         read(1, 0, read_a)
+        round_wc(0)
         read(1, 1, read_b, read_a)
         cues(0, 1, lambda: quantise_h(0, 0))
         clear_beside(1, 32768)
-        cues(1, 0, lambda: (round_wc(0, nc.vector.tensor_copy), quantise_h(0, 1)))
+        cues(1, 0, lambda: quantise_h(0, 1))
         clear_beside(2, 16384)
         quantise_wc(0)
         quantise_h(1, 0, parts=2)
@@ -339,7 +340,7 @@ def tile_list_baggage_density_cues_kernel(
 
         for i in range(2):
             mix(i, 0)
-        round_wc(1, nc.scalar.copy)
+        round_wc(1)
         for i in range(2):
             scatter(i, 0, HALF)
         quantise_wc(1)

@@ -131,19 +131,21 @@ def tile_list_baggage_density_cues_kernel(
                 wbw_raw[:].rearrange("p (a m t u) -> p a t m u", a=PASSES, t=4, u=2),
             )
 
-        gains = banks.tile([P, PASSES, P], F32, name="gains", offset=2048 * 7)
+        gains = banks.tile([P, 4, P], F32, name="gains", offset=2048 * 7)
 
         def load_gains():
             identity = held("identity", [P, P], F32)
             make_identity(nc, identity[:])
-            gain_rows = held("gain_rows", [P, PASSES * P], F32)
+            gain_rows = held("gain_rows", [P, 512], F32)
             nc.gpsimd.memset(gain_rows[:], 0.0)
-            nc.sync.dma_start(
-                out=gain_rows[0:4, :].rearrange("t (m u) -> t m u", u=4),
-                in_=gain.rearrange("(m t u) -> t m u", t=4, u=4),
+            nc.sync.dma_start(out=gain_rows[0:PASSES, :], in_=gain.rearrange("(b c) -> b c", b=PASSES))
+            gain_dealt = held("gain_dealt", [P, 512], F32)
+            nc.scalar.copy(
+                gain_dealt[:].rearrange("p (t m u) -> p t m u", t=4, u=4),
+                gain_rows[:].rearrange("p (m t u) -> p t m u", t=4, u=4),
             )
-            for b in range(PASSES):
-                nc.tensor.transpose(gains[:, b, :], gain_rows[:, P * b : P * (b + 1)], identity[:])
+            for t in range(4):
+                nc.tensor.transpose(gains[:, t, :], gain_dealt[:, P * t : P * (t + 1)], identity[:])
 
         wa_bf, wa_q, wa_s = {}, {}, {}
 
@@ -241,7 +243,7 @@ def tile_list_baggage_density_cues_kernel(
                     "p (c i t) -> p c t i", i=4, t=4
                 ),
                 ea[b, half][:, :, QUART * part : QUART * (part + 1)].rearrange("p t (c i) -> p c t i", i=4),
-                gains[:, b, 0:4].unsqueeze(1).unsqueeze(3).to_broadcast([P, QUART // 4, 4, 4]),
+                gains[:, :, b : b + 1].unsqueeze(1).to_broadcast([P, QUART // 4, 4, 4]),
                 ALU.mult,
             )
 

@@ -21,6 +21,7 @@ P = 128
 PASSES = 2
 HALF = S // 2
 QUART = S // 4
+SHARE = 768
 WA_BF_AT = {(0, 0): 65536, (1, 0): 40960, (0, 1): 57344, (1, 1): 24576}
 EB_AT = {(0, 0): 69632, (0, 1): 77824, (1, 0): 40960, (1, 1): 57344}
 
@@ -172,7 +173,7 @@ def tile_list_baggage_density_cues_kernel(
         wc_bf, wc_q, wc_s = {}, {}, {}
 
         def round_wc(pair):
-            wc_bf[pair] = placed(f"wc_bf{pair}", (90112, 86016)[pair], [P, PASSES, 1024], BF16)
+            wc_bf[pair] = placed(f"wc_bf{pair}", (90112, 83968)[pair], [P, PASSES, 1024], BF16)
             for b in range(PASSES):
                 nc.scalar.copy(
                     wc_bf[pair][:, b, :].rearrange("p (e q t) -> p q e t", e=2, t=4),
@@ -229,11 +230,15 @@ def tile_list_baggage_density_cues_kernel(
                     reading(b, half, t)
 
         def subtract(b, half, part):
-            if b == half:
-                where = (slice(None), slice(2 * part, 2 * part + 2), slice(None))
-            else:
-                where = (slice(None), slice(None), slice(QUART * part, QUART * (part + 1)))
+            where = (slice(None), slice(2 * part, 2 * part + 2), slice(None))
             nc.vector.tensor_tensor(ea[b, half][where], ea[b, half][where], eb[b, half][where], ALU.subtract)
+
+        def subtract_shared(b, half, before):
+            difference = placed(f"difference{b}{half}", EB_AT[before], [P, 4, HALF], F32)
+            views = [tile[:].rearrange("p t j -> p (t j)") for tile in (difference, ea[b, half], eb[b, half])]
+            nc.gpsimd.tensor_tensor(*[view[:, 0:SHARE] for view in views], ALU.subtract)
+            nc.vector.tensor_tensor(*[view[:, SHARE:] for view in views], ALU.subtract)
+            ea[b, half] = difference
 
         def scale(b, half, part):
             if part == 0:
@@ -292,22 +297,28 @@ def tile_list_baggage_density_cues_kernel(
         nc.sync.dma_start(out=weights[:], in_=wgo)
         quantise_wa(0, 1)
         cues(0, 0, lambda: round_wa(1, 1, nc.vector.tensor_copy), lambda: quantise_wa(1, 1))
-        clear_beside(0, 24576)
         read(1, 0, read_b)
         read(1, 0, read_a)
         round_wc(0)
         read(1, 1, read_b, read_a)
-        cues(0, 1, lambda: quantise_h(0, 0))
-        clear_beside(1, 32768)
-        cues(1, 0, lambda: quantise_h(0, 1))
-        clear_beside(2, 16384)
+        subtract_shared(0, 1, (0, 0))
+        quantise_h(0, 0)
+        scale(0, 1, 0)
+        scale(0, 1, 1)
+        subtract_shared(1, 0, (0, 1))
+        quantise_h(0, 1)
+        scale(1, 0, 0)
+        scale(1, 0, 1)
         quantise_wc(0)
         quantise_h(1, 0, parts=2)
-        clear_beside(3, 49152)
-        cues(1, 1, lambda: None)
+        subtract_shared(1, 1, (1, 0))
+        clear_beside(0, 49152)
+        scale(1, 1, 0)
+        scale(1, 1, 1)
         quantise_h(1, 1, parts=2)
+        clear_beside(1, 88064)
 
-        ys = [held(f"y{pair}", [P, 2, S], F32) for pair in range(2)]
+        ys = [placed(f"y{pair}", (24576, 16384)[pair], [P, 2, S], F32) for pair in range(2)]
 
         def mix(i, half):
             pair, e = divmod(i, 2)
@@ -346,9 +357,11 @@ def tile_list_baggage_density_cues_kernel(
         for i in range(2):
             scatter(i, 0, HALF)
         quantise_wc(1)
+        clear_beside(2, 77824)
         for i in range(2):
             mix(i, 1)
             scatter(i, HALF, S)
+        clear_beside(3, 24576)
         for i in range(2, 4):
             for half in range(2):
                 mix(i, half)

@@ -58,23 +58,23 @@ def tile_list_baggage_density_cues_kernel(
         wbs_raw = held("wbs_raw", [P, H], U8)
         nc.gpsimd.memset(tscale[:].bitcast(I32), 0)
         nc.vector.memset(wbs_raw[:].bitcast(I32), 0)
+        twords = [placed("twords0", 8192, [P, T], U32), reused("twords1", "tab1", [P, T], U32)]
+
+        def load_table(a, c0=0, c1=T):
+            nc.sync.dma_start(
+                out=twords[a][:, c0:c1].bitcast(I32),
+                in_=tab_words[a].rearrange("p t i -> p (t i)").bitcast(I32)[:, c0:c1],
+            )
+
         nc.sync.dma_start(pick[:], offs)
-        nc.sync.dma_start(place[:], offs2)
+        load_table(0, 0, T // 4)
         nc.sync.dma_start(
             out=tscale[0:P:4, :].bitcast(I32), in_=tab_scales.bitcast(I32).rearrange("a q t -> q a t")
         )
         nc.sync.dma_start(
             out=wbs_raw[0:P:4, :].bitcast(I32), in_=wb_scales.bitcast(I32).rearrange("a q c -> q a c")
         )
-        twords = [placed("twords0", 8192, [P, T], U32), reused("twords1", "tab1", [P, T], U32)]
-
-        def load_table(a):
-            nc.sync.dma_start(
-                out=twords[a][:].bitcast(I32),
-                in_=tab_words[a].rearrange("p t i -> p (t i)").bitcast(I32),
-            )
-
-        load_table(0)
+        load_table(0, T // 4, T)
         wbw_raw = reused("wbw_raw", "wb", [P, PASSES * H // 2], I32)
         nc.sync.dma_start(
             out=wbw_raw[:].rearrange("p (a c) -> p a c", a=PASSES),
@@ -240,17 +240,16 @@ def tile_list_baggage_density_cues_kernel(
             nc.vector.tensor_tensor(*[view[:, SHARE:] for view in views], ALU.subtract)
             ea[b, half] = difference
 
-        def scale(b, half, part):
-            if part == 0:
-                hb[b, half] = placed(f"hb{b}{half}", (32768, 16384, 49152, 86016)[2 * b + half], [P, 4 * HALF], BF16)
-            nc.vector.tensor_tensor(
-                hb[b, half][:, 4 * QUART * part : 4 * QUART * (part + 1)].rearrange(
-                    "p (c i t) -> p c t i", i=4, t=4
-                ),
-                ea[b, half][:, :, QUART * part : QUART * (part + 1)].rearrange("p t (c i) -> p c t i", i=4),
-                gains[:, :, b : b + 1].unsqueeze(1).to_broadcast([P, QUART // 4, 4, 4]),
-                ALU.mult,
-            )
+        def scale(b, half, parts=1):
+            hb[b, half] = placed(f"hb{b}{half}", (32768, 16384, 49152, 86016)[2 * b + half], [P, 4 * HALF], BF16)
+            width = HALF // parts
+            for c0 in range(0, HALF, width):
+                nc.vector.tensor_tensor(
+                    hb[b, half][:, 4 * c0 : 4 * (c0 + width)].rearrange("p (c i t) -> p c t i", i=4, t=4),
+                    ea[b, half][:, :, c0 : c0 + width].rearrange("p t (c i) -> p c t i", i=4),
+                    gains[:, :, b : b + 1].unsqueeze(1).to_broadcast([P, width // 4, 4, 4]),
+                    ALU.mult,
+                )
 
         def quantise_h(b, half, parts=1):
             h_q[b, half] = held(f"h_q{b}{half}", [P, HALF], U32)
@@ -268,8 +267,7 @@ def tile_list_baggage_density_cues_kernel(
             between()
             subtract(b, half, 1)
             later()
-            scale(b, half, 0)
-            scale(b, half, 1)
+            scale(b, half)
 
         gather(0, 0)
         gather(0, 1)
@@ -293,6 +291,7 @@ def tile_list_baggage_density_cues_kernel(
         read(0, 1, read_b, codes=range(2, 4))
         read(0, 1, read_a)
         round_wa(0, 1, nc.vector.tensor_copy)
+        nc.sync.dma_start(place[:], offs2)
         weights = reused("weights", "wb", [P, S], F32)
         nc.sync.dma_start(out=weights[:], in_=wgo)
         quantise_wa(0, 1)
@@ -303,18 +302,15 @@ def tile_list_baggage_density_cues_kernel(
         read(1, 1, read_b, read_a)
         subtract_shared(0, 1, (0, 0))
         quantise_h(0, 0)
-        scale(0, 1, 0)
-        scale(0, 1, 1)
+        scale(0, 1)
         subtract_shared(1, 0, (0, 1))
         quantise_h(0, 1)
-        scale(1, 0, 0)
-        scale(1, 0, 1)
+        scale(1, 0)
         quantise_wc(0)
-        quantise_h(1, 0, parts=2)
+        quantise_h(1, 0)
         subtract_shared(1, 1, (1, 0))
         clear_beside(0, 49152)
-        scale(1, 1, 0)
-        scale(1, 1, 1)
+        scale(1, 1, parts=2)
         quantise_h(1, 1, parts=2)
         clear_beside(1, 88064)
 

@@ -350,15 +350,16 @@ def tile_list_baggage_density_cues_kernel(
         for i in range(2):
             mix(i, 0)
         round_wc(1)
+        clear_beside(3, 0)
         for i in range(2):
             scatter(i, 0, HALF)
         quantise_wc(1)
         clear_beside(2, 77824)
-        for i in range(2):
+        mix(0, 1)
+        scatter(0, HALF, S)
+        for i in range(2, 4):
+            mix(i, 0)
+            scatter(i, 0, HALF)
+        for i in range(1, 4):
             mix(i, 1)
             scatter(i, HALF, S)
-        clear_beside(3, 24576)
-        for i in range(2, 4):
-            for half in range(2):
-                mix(i, half)
-            scatter(i, 0, S)

@@ -20,10 +20,9 @@ ALU = mybir.AluOpType
 P = 128
 PASSES = 2
 HALF = S // 2
-QUART = S // 4
+KIB = 1024
 SHARE = 768
-WA_BF_AT = {(0, 0): 65536, (1, 0): 40960, (0, 1): 57344, (1, 1): 24576}
-EB_AT = {(0, 0): 69632, (0, 1): 77824, (1, 0): 40960, (1, 1): 57344}
+FIRST = 768
 
 
 def tile_list_baggage_density_cues_kernel(
@@ -37,28 +36,43 @@ def tile_list_baggage_density_cues_kernel(
         banks = ctx.enter_context(tc.psum_pool(name="banks", bufs=1))
         taken = []
 
-        def next_bank():
-            k = len(taken)
+        def take_bank(k):
             taken.append(k)
-            return banks.tile([P, HALF], F32, name=f"bank{k}", offset=2048 * (k % 7))
+            return banks.tile([P, HALF], F32, name=f"bank{len(taken)}", offset=2048 * k)
 
         def held(name, shape, dtype):
             return keep.tile(shape, dtype, name=name, align_bytes=64)
 
-        def reused(name, tag, shape, dtype):
-            return keep.tile(shape, dtype, name=name, tag=tag, align_bytes=64)
-
-        def placed(name, offset, shape, dtype):
-            return arena.tile(shape, dtype, name=name, offset=offset, align_bytes=64)
+        def placed(name, kib, shape, dtype):
+            return arena.tile(shape, dtype, name=name, offset=kib * KIB, align_bytes=64)
 
         pick = lists.tile([P, S // 16], U16, name="pick")
         place = lists.tile([P, S // 16], U16, name="place")
 
         tscale = placed("tscale", 0, [P, T], U8)
-        wbs_raw = held("wbs_raw", [P, H], U8)
+        wbs_raw = held("wbs_raw", [P, H // 4], U32)
+        gain_rows = held("gain_rows", [P, 512], F32)
+        planes = held("planes", [P, PASSES, S + H], U8)
+        pages = {}
+
+        def clear(i, kib):
+            pages[i] = placed(f"page{i}", kib, [P, T2], F32)
+            nc.gpsimd.memset(pages[i][:].bitcast(I32), 0)
+
+        def clear_on_one_port(words):
+            count = words.shape[1]
+            nc.vector.memset(words[:, 0 : count // 2 - 1], 0)
+            nc.vector.memset(words[:, count // 2 - 1 :], 0)
+
         nc.gpsimd.memset(tscale[:].bitcast(I32), 0)
-        nc.vector.memset(wbs_raw[:].bitcast(I32), 0)
-        twords = [placed("twords0", 8192, [P, T], U32), reused("twords1", "tab1", [P, T], U32)]
+        clear_on_one_port(wbs_raw[:].bitcast(I32))
+        clear_on_one_port(gain_rows[:].bitcast(I32))
+        clear_on_one_port(planes[:].rearrange("p a c -> p (a c)").bitcast(I32))
+        identity = held("identity", [P, P], F32)
+        make_identity(nc, identity[:])
+        clear(1, 124)
+
+        twords = [placed("twords0", 8, [P, T], U32), placed("twords1", 24, [P, T], U32)]
 
         def load_table(a, c0=0, c1=T):
             nc.sync.dma_start(
@@ -74,111 +88,94 @@ def tile_list_baggage_density_cues_kernel(
         nc.sync.dma_start(
             out=wbs_raw[0:P:4, :].bitcast(I32), in_=wb_scales.bitcast(I32).rearrange("a q c -> q a c")
         )
+        nc.sync.dma_start(out=gain_rows[0:PASSES, :], in_=gain.rearrange("(b c) -> b c", b=PASSES))
         load_table(0, T // 4, T)
-        wbw_raw = reused("wbw_raw", "wb", [P, PASSES * H // 2], I32)
+        wbw_raw = placed("wbw_raw", 16, [P, PASSES * H // 2], U32)
         nc.sync.dma_start(
-            out=wbw_raw[:].rearrange("p (a c) -> p a c", a=PASSES),
+            out=wbw_raw[:].bitcast(I32).rearrange("p (a c) -> p a c", a=PASSES),
             in_=wb_words.bitcast(I32).rearrange("a p c -> p a c"),
         )
         load_table(1)
 
-        planes = held("planes", [P, PASSES, S + H], U8)
-        nc.vector.memset(planes[:].rearrange("p a c -> p (a c)").bitcast(I32), 0)
-        pages = {}
-
-        def clear_beside(i, offset):
-            pages[i] = placed(f"page{i}", offset, [P, T2], F32)
-            nc.gpsimd.memset(pages[i][:].bitcast(I32), 0)
-
-        rows_in = reused("rows_in", "small", [P, S + H], U8)
-        nc.vector.tensor_copy(
-            rows_in[:, S:].bitcast(I32).rearrange("p (t m) -> p t m", t=4),
-            wbs_raw[:].bitcast(I32).rearrange("p (m t) -> p t m", t=4),
+        rows_in = held("rows_in", [P, (S + H) // 4], U32)
+        nc.scalar.copy(
+            rows_in[:, S // 4 :].rearrange("p (t m) -> p t m", t=4),
+            wbs_raw[:].rearrange("p (m t) -> p t m", t=4),
         )
-        gscale = held("gscale", [P, S], U8)
+        gscale = placed("gscale", 2, [P, S], U8)
         nc.vector.tensor_copy(gscale[:], tscale[:].indirect(pick[:]))
-        nc.vector.tensor_copy(rows_in[:, 0:S].bitcast(I32), gscale[:].bitcast(I32))
+        nc.vector.tensor_copy(rows_in[:, 0 : S // 4], gscale[:].bitcast(U32))
         for d in range(4):
             nc.sync.dma_start(
                 out=planes[32 * d : 32 * d + 4, :, :].rearrange("p a c -> p (a c)").bitcast(I32),
                 in_=rows_in[32 * d : 32 * (d + 1) : 4, :].bitcast(I32),
             )
 
-        wa_raw = {}
+        wbw = held("wbw", [P, PASSES * H // 2], U32)
+        wbw_bytes = wbw[:].bitcast(U8)
+        nc.scalar.copy(
+            wbw[:].rearrange("p (a t m u) -> p a t m u", a=PASSES, t=4, u=2),
+            wbw_raw[:].rearrange("p (a m t u) -> p a t m u", a=PASSES, t=4, u=2),
+        )
 
-        def load_wa(a, b, tile):
-            wa_raw[a, b] = tile
+        gains = banks.tile([P, 4, P], F32, name="gains", offset=2048 * 7)
+        gain_dealt = held("gain_dealt", [P, 512], F32)
+        nc.scalar.activation(
+            gain_dealt[:].rearrange("p (t m u) -> p t m u", t=4, u=4),
+            gain_rows[:].rearrange("p (m t u) -> p t m u", t=4, u=4),
+            ACT.Copy,
+        )
+        for t in range(4):
+            nc.tensor.transpose(gains[:, t, :], gain_dealt[:, P * t : P * (t + 1)], identity[:])
+        gain_run = held("gain_run", [P, 64, 4], F32)
+        nc.scalar.copy(gain_run[:], gains[:, :, 1:2].rearrange("p t o -> p o t").to_broadcast([P, 64, 4]))
+
+        wa_raw, wa_q, wa_s = {}, {}, {}
+
+        def load_wa(a, b):
+            wa_raw[a, b] = placed(f"wa_raw{a}{b}", 8 * (a + 2 * b), [P, 4, 512], F32)
             nc.sync.dma_start(
-                out=tile[:],
+                out=wa_raw[a, b][:],
                 in_=wa[512 * a : 512 * (a + 1), 512 * b : 512 * (b + 1)].rearrange("(p i) c -> p i c", i=4),
             )
 
-        load_wa(0, 0, placed("wa_raw00", 0, [P, 4, 512], F32))
+        def quantise_wa(a, b):
+            rounded = placed(f"wa_bf{a}{b}", (32, 36, 40, 50)[a + 2 * b], [P, 2048], BF16)
+            for t in (0, 2):
+                nc.vector.tensor_copy(
+                    rounded[:].rearrange("p (t m u i) -> p t m i u", t=4, u=4, i=4)[:, t : t + 2],
+                    wa_raw[a, b][:].rearrange("p i (m t u) -> p t m i u", t=4, u=4)[:, t : t + 2],
+                )
+            wa_q[a, b] = held(f"wa_q{a}{b}", [P, 512], U32)
+            wa_s[a, b] = held(f"wa_s{a}{b}", [P, 512], U8)
+            for c in (0, 256):
+                nc.vector.quantize_mx(
+                    out=wa_q[a, b][:, c : c + 256].bitcast(E4M3),
+                    scales=wa_s[a, b][:, c : c + 256],
+                    in_=rounded[:, 4 * c : 4 * c + 1024],
+                )
 
         vwords = {}
 
-        def gather(a, half):
-            vwords[a, half] = held(f"vwords{a}{half}", [P, HALF], U32)
-            nc.vector.tensor_copy(
-                vwords[a, half][:], twords[a][:].indirect(pick[:, 32 * half : 32 * (half + 1)])
-            )
+        def gather(a, half, tile):
+            vwords[a, half] = tile
+            nc.vector.tensor_copy(tile[:], twords[a][:].indirect(pick[:, 32 * half : 32 * (half + 1)]))
 
-        wbw = held("wbw", [P, PASSES * H // 2], I32)
-        wbw_bytes = wbw[:].bitcast(U8)
+        wc_raw, wc_bf, wc_q, wc_s = {}, {}, {}, {}
 
-        def order_wb():
-            nc.vector.tensor_copy(
-                wbw[:].rearrange("p (a t m u) -> p a t m u", a=PASSES, t=4, u=2),
-                wbw_raw[:].rearrange("p (a m t u) -> p a t m u", a=PASSES, t=4, u=2),
-            )
-
-        gains = banks.tile([P, 4, P], F32, name="gains", offset=2048 * 7)
-
-        def load_gains():
-            identity = held("identity", [P, P], F32)
-            make_identity(nc, identity[:])
-            gain_rows = held("gain_rows", [P, 512], F32)
-            nc.gpsimd.memset(gain_rows[:], 0.0)
-            nc.sync.dma_start(out=gain_rows[0:PASSES, :], in_=gain.rearrange("(b c) -> b c", b=PASSES))
-            gain_dealt = held("gain_dealt", [P, 512], F32)
-            nc.scalar.copy(
-                gain_dealt[:].rearrange("p (t m u) -> p t m u", t=4, u=4),
-                gain_rows[:].rearrange("p (m t u) -> p t m u", t=4, u=4),
-            )
-            for t in range(4):
-                nc.tensor.transpose(gains[:, t, :], gain_dealt[:, P * t : P * (t + 1)], identity[:])
-
-        wa_bf, wa_q, wa_s = {}, {}, {}
-
-        def round_wa(a, b, copy):
-            wa_bf[a, b] = placed(f"wa_bf{a}{b}", WA_BF_AT[a, b], [P, 2048], BF16)
-            copy(
-                wa_bf[a, b][:].rearrange("p (t m u i) -> p t m i u", t=4, u=4, i=4),
-                wa_raw[a, b][:].rearrange("p i (m t u) -> p t m i u", t=4, u=4),
-            )
-
-        def quantise_wa(a, b):
-            wa_q[a, b] = held(f"wa_q{a}{b}", [P, 512], U32)
-            wa_s[a, b] = held(f"wa_s{a}{b}", [P, 512], U8)
-            nc.vector.quantize_mx(out=wa_q[a, b][:].bitcast(E4M3), scales=wa_s[a, b][:], in_=wa_bf[a, b][:])
-
-        wc_raw = {}
-
-        def load_wc(b, tile):
-            wc_raw[b] = tile
+        def load_wc(b):
+            wc_raw[b] = placed(f"wc_raw{b}", 8 * b, [P, 4, N], F32)
             rows = wc[512 * b : 512 * (b + 1), :].rearrange("(m t u) n -> t m u n", t=4, u=4)
             for t in range(4):
-                nc.sync.dma_start(out=tile[:, t, :], in_=rows[t])
+                nc.sync.dma_start(out=wc_raw[b][:, t, :], in_=rows[t])
 
-        wc_bf, wc_q, wc_s = {}, {}, {}
-
-        def round_wc(pair):
-            wc_bf[pair] = placed(f"wc_bf{pair}", (90112, 83968)[pair], [P, PASSES, 1024], BF16)
-            for b in range(PASSES):
-                nc.scalar.copy(
-                    wc_bf[pair][:, b, :].rearrange("p (e q t) -> p q e t", e=2, t=4),
-                    wc_raw[b][:].rearrange("p t (q i) -> p q i t", i=4)[:, :, 2 * pair : 2 * pair + 2, :],
-                )
+        def round_wc(pair, b):
+            if b == 0:
+                wc_bf[pair] = placed(f"wc_bf{pair}", 16 + 4 * pair, [P, PASSES, 1024], BF16)
+            nc.scalar.copy(
+                wc_bf[pair][:, b, :].rearrange("p (e q t) -> p q e t", e=2, t=4),
+                wc_raw[b][:].rearrange("p t (q i) -> p q i t", i=4)[:, :, 2 * pair : 2 * pair + 2, :],
+            )
 
         def quantise_wc(pair):
             wc_q[pair] = held(f"wc_q{pair}", [P, 512], U32)
@@ -189,136 +186,90 @@ def tile_list_baggage_density_cues_kernel(
                 in_=wc_bf[pair][:].rearrange("p b c -> p (b c)"),
             )
 
-        ea, eb, hb, h_q, h_s = {}, {}, {}, {}, {}
-
-        def read_a(b, half, t):
-            if t == 0:
-                ea[b, half] = held(f"ea{b}{half}", [P, 4, HALF], F32)
-            bank = next_bank()
-            for a in range(PASSES):
-                nc.tensor.matmul_mx(
-                    out=bank[:],
-                    lhsT=wa_q[a, b][:, P * t : P * (t + 1)].bitcast(E4M3),
-                    lhsT_scale=wa_s[a, b][:, P * t : P * (t + 1)],
-                    rhs=vwords[a, half][:].bitcast(E4M3),
-                    rhs_scale=planes[:, a, half * HALF : (half + 1) * HALF],
-                    start=(a == 0),
-                    stop=(a == PASSES - 1),
-                )
-            nc.scalar.activation(ea[b, half][:, t, :], bank[:], ACT.Exp)
-
-        def read_b(b, half, t):
-            if t == 0:
-                eb[b, half] = placed(f"eb{b}{half}", EB_AT[b, half], [P, 4, HALF], F32)
-            bank = next_bank()
+        def operands(reading, a, b, t):
+            if reading == "a":
+                cols = slice(P * t, P * (t + 1))
+                return wa_q[a, b][:, cols].bitcast(E4M3), wa_s[a, b][:, cols]
             col = t * 256 + b * P
+            codes = wbw_bytes[:, 2 * (a * H + col) : 2 * (a * H + col + P)]
+            return codes.bitcast(E2M1), planes[:, a, S + col : S + col + P]
+
+        def multiply(bank, reading, b, t, j0, width):
+            half, c0 = divmod(j0, HALF)
             for a in range(PASSES):
+                codes, scales = operands(reading, a, b, t)
                 nc.tensor.matmul_mx(
-                    out=bank[:],
-                    lhsT=wbw_bytes[:, 2 * (a * H + col) : 2 * (a * H + col + P)].bitcast(E2M1),
-                    lhsT_scale=planes[:, a, S + col : S + col + P],
-                    rhs=vwords[a, half][:].bitcast(E4M3),
-                    rhs_scale=planes[:, a, half * HALF : (half + 1) * HALF],
+                    out=bank,
+                    lhsT=codes,
+                    lhsT_scale=scales,
+                    rhs=vwords[a, half][:, c0 : c0 + width].bitcast(E4M3),
+                    rhs_scale=planes[:, a, j0 : j0 + width],
                     start=(a == 0),
                     stop=(a == PASSES - 1),
                 )
-            nc.scalar.activation(eb[b, half][:, t, :], bank[:], ACT.Exp)
 
-        def read(b, half, *readings, codes=range(4)):
-            for t in codes:
-                for reading in readings:
-                    reading(b, half, t)
+        exps, difference, hb, h_q, h_s = {}, {}, {}, {}, {}
+        exps_at = {"a": (60, 76, 92, 108), "b": (68, 84, 100, 116)}
 
-        def subtract(b, half, part):
-            where = (slice(None), slice(2 * part, 2 * part + 2), slice(None))
-            nc.vector.tensor_tensor(ea[b, half][where], ea[b, half][where], eb[b, half][where], ALU.subtract)
+        def exp_tile(reading, b, half):
+            exps[reading, b, half] = placed(
+                f"e{reading}{b}{half}", exps_at[reading][b + 2 * half], [P, 4 * HALF], F32
+            )
+            return exps[reading, b, half]
 
-        def subtract_shared(b, half, before):
-            difference = placed(f"difference{b}{half}", EB_AT[before], [P, 4, HALF], F32)
-            views = [tile[:].rearrange("p t j -> p (t j)") for tile in (difference, ea[b, half], eb[b, half])]
-            nc.gpsimd.tensor_tensor(*[view[:, 0:SHARE] for view in views], ALU.subtract)
-            nc.vector.tensor_tensor(*[view[:, SHARE:] for view in views], ALU.subtract)
-            ea[b, half] = difference
+        def read(reading, b, half, ring):
+            tile = exp_tile(reading, b, half)
+            for t in range(4):
+                bank = take_bank(ring[t])
+                multiply(bank[:], reading, b, t, HALF * half, HALF)
+                nc.scalar.activation(tile[:, HALF * t : HALF * (t + 1)], bank[:], ACT.Exp)
 
-        def scale(b, half, parts=1):
-            hb[b, half] = placed(f"hb{b}{half}", (32768, 16384, 49152, 86016)[2 * b + half], [P, 4 * HALF], BF16)
-            width = HALF // parts
-            for c0 in range(0, HALF, width):
-                nc.vector.tensor_tensor(
-                    hb[b, half][:, 4 * c0 : 4 * (c0 + width)].rearrange("p (c i t) -> p c t i", i=4, t=4),
-                    ea[b, half][:, :, c0 : c0 + width].rearrange("p t (c i) -> p c t i", i=4),
-                    gains[:, :, b : b + 1].unsqueeze(1).to_broadcast([P, width // 4, 4, 4]),
-                    ALU.mult,
-                )
+        def read_woven(b, half, ring):
+            tiles = {reading: exp_tile(reading, b, half) for reading in "ba"}
+            for c in range(4):
+                for k, reading in enumerate("ba"):
+                    bank = take_bank(ring[(2 * c + k) % len(ring)])
+                    for t in range(4):
+                        multiply(bank[:, P * t : P * (t + 1)], reading, b, t, HALF * half + P * c, P)
+                    nc.scalar.activation(
+                        tiles[reading][:, HALF * c : HALF * (c + 1)].rearrange("p (j t) -> p j t", t=4),
+                        bank[:].rearrange("p (t j) -> p j t", t=4),
+                        ACT.Exp,
+                    )
 
-        def quantise_h(b, half, parts=1):
+        def subtract(engine, b, half, c0, c1, kib=None):
+            if kib is not None:
+                difference[b, half] = placed(f"difference{b}{half}", kib, [P, 4 * HALF], F32)
+            views = (difference[b, half], exps["a", b, half], exps["b", b, half])
+            engine.tensor_tensor(*[view[:, c0:c1] for view in views], ALU.subtract)
+
+        def scale(b, half, kib):
+            hb[b, half] = placed(f"hb{b}{half}", kib, [P, 4 * HALF], BF16)
+            nc.vector.tensor_tensor(
+                hb[b, half][:].rearrange("p (c i t) -> p c t i", i=4, t=4),
+                difference[b, half][:].rearrange("p (t c i) -> p c t i", t=4, i=4),
+                gains[:, :, b : b + 1].unsqueeze(1).to_broadcast([P, HALF // 4, 4, 4]),
+                ALU.mult,
+            )
+
+        def scale_woven(b, half, c0, c1):
+            nc.gpsimd.tensor_tensor(
+                hb[b, half][:, c0:c1].rearrange("p (g c) -> p g c", c=256),
+                difference[b, half][:, c0:c1].rearrange("p (g c) -> p g c", c=256),
+                gain_run[:].rearrange("p j t -> p (j t)").unsqueeze(1).to_broadcast([P, (c1 - c0) // 256, 256]),
+                ALU.mult,
+            )
+
+        def quantise_h(b, half):
             h_q[b, half] = held(f"h_q{b}{half}", [P, HALF], U32)
             h_s[b, half] = held(f"h_s{b}{half}", [P, HALF], U8)
-            width = HALF // parts
-            for c0 in range(0, HALF, width):
-                nc.vector.quantize_mx(
-                    out=h_q[b, half][:, c0 : c0 + width].bitcast(E4M3),
-                    scales=h_s[b, half][:, c0 : c0 + width],
-                    in_=hb[b, half][:, 4 * c0 : 4 * (c0 + width)],
-                )
+            nc.vector.quantize_mx(out=h_q[b, half][:].bitcast(E4M3), scales=h_s[b, half][:], in_=hb[b, half][:])
 
-        def cues(b, half, between, later=lambda: None):
-            subtract(b, half, 0)
-            between()
-            subtract(b, half, 1)
-            later()
-            scale(b, half)
+        squares, ys = {}, {}
 
-        gather(0, 0)
-        gather(0, 1)
-        load_wa(1, 0, placed("wa_raw10", 8192, [P, 4, 512], F32))
-        order_wb()
-        load_wa(0, 1, reused("wa_raw01", "wb", [P, 4, 512], F32))
-        gather(1, 0)
-        read(0, 0, read_b)
-        gather(1, 1)
-        load_wa(1, 1, reused("wa_raw11", "tab1", [P, 4, 512], F32))
-        read(0, 1, read_b, codes=range(2))
-        load_gains()
-        round_wa(0, 0, nc.vector.tensor_copy)
-        load_wc(0, placed("wc_raw0", 0, [P, 4, N], F32))
-        quantise_wa(0, 0)
-        round_wa(1, 0, nc.vector.tensor_copy)
-        load_wc(1, placed("wc_raw1", 8192, [P, 4, N], F32))
-        quantise_wa(1, 0)
-        read(0, 0, read_a)
-        taken.extend(range(3))
-        read(0, 1, read_b, codes=range(2, 4))
-        read(0, 1, read_a)
-        round_wa(0, 1, nc.vector.tensor_copy)
-        nc.sync.dma_start(place[:], offs2)
-        weights = reused("weights", "wb", [P, S], F32)
-        nc.sync.dma_start(out=weights[:], in_=wgo)
-        quantise_wa(0, 1)
-        cues(0, 0, lambda: round_wa(1, 1, nc.vector.tensor_copy), lambda: quantise_wa(1, 1))
-        read(1, 0, read_b)
-        read(1, 0, read_a)
-        round_wc(0)
-        read(1, 1, read_b, read_a)
-        subtract_shared(0, 1, (0, 0))
-        quantise_h(0, 0)
-        scale(0, 1)
-        subtract_shared(1, 0, (0, 1))
-        quantise_h(0, 1)
-        scale(1, 0)
-        quantise_wc(0)
-        quantise_h(1, 0)
-        subtract_shared(1, 1, (1, 0))
-        clear_beside(0, 49152)
-        scale(1, 1, parts=2)
-        quantise_h(1, 1, parts=2)
-        clear_beside(1, 88064)
-
-        ys = [placed(f"y{pair}", (24576, 16384)[pair], [P, 2, S], F32) for pair in range(2)]
-
-        def mix(i, half):
+        def mix(i, half, kib):
             pair, e = divmod(i, 2)
-            bank = next_bank()
+            bank = take_bank((1, 3, 4)[len(squares) % 3])
             for b in range(PASSES):
                 col = 256 * b + P * e
                 nc.tensor.matmul_mx(
@@ -330,36 +281,101 @@ def tile_list_baggage_density_cues_kernel(
                     start=(b == 0),
                     stop=(b == PASSES - 1),
                 )
-            y = ys[pair][:, e, HALF * half : HALF * (half + 1)]
-            nc.scalar.activation(y, bank[:], ACT.Square)
-            nc.scalar.activation(y, y, ACT.Ln, bias=1.0)
+            squares[i, half] = placed(f"square{i}{half}", kib, [P, HALF], F32)
+            nc.scalar.activation(squares[i, half][:], bank[:], ACT.Square)
+
+        def logarithm(i, half, kib=None):
+            ys[i, half] = squares[i, half] if kib is None else placed(f"y{i}{half}", kib, [P, HALF], F32)
+            nc.scalar.activation(ys[i, half][:], squares[i, half][:], ACT.Ln, bias=1.0)
 
         rows = out.rearrange("(p i) t -> i p t", i=4)
 
-        def scatter(i, j0, j1):
-            pair, e = divmod(i, 2)
-            nc.vector.tensor_tensor(
-                pages[i][:].indirect(place[:, j0 // 16 : j1 // 16]),
-                ys[pair][:, e, j0:j1],
-                weights[:, j0:j1],
-                ALU.mult,
-            )
-            if j1 == S:
-                nc.sync.dma_start(out=rows[i], in_=pages[i][:])
+        def slots(i, half):
+            return pages[i][:].indirect(place[:, 32 * half : 32 * (half + 1)])
 
-        for i in range(2):
-            mix(i, 0)
-        round_wc(1)
-        clear_beside(3, 0)
-        for i in range(2):
-            scatter(i, 0, HALF)
+        def scatter(i, half):
+            nc.vector.tensor_tensor(
+                slots(i, half), ys[i, half][:], weights[:, HALF * half : HALF * (half + 1)], ALU.mult
+            )
+
+        weighted = {}
+
+        def weigh(engine, i, kib):
+            weighted[i] = placed(f"weighted{i}", kib, [P, HALF], F32)
+            engine.tensor_tensor(weighted[i][:], ys[i, 0][:], weights[:, 0:HALF], ALU.mult)
+
+        def scatter_copy(i):
+            nc.vector.tensor_copy(slots(i, 0), weighted[i][:])
+
+        load_wa(0, 0)
+        gather(0, 0, held("vwords00", [P, HALF], U32))
+        gather(0, 1, held("vwords01", [P, HALF], U32))
+        load_wa(1, 0)
+        load_wa(0, 1)
+        gather(1, 0, held("vwords10", [P, HALF], U32))
+        read("b", 0, 0, (0, 1, 2, 3))
+        gather(1, 1, placed("vwords11", 160, [P, HALF], U32))
+        load_wa(1, 1)
+        read("b", 1, 0, (4, 5, 6, 0))
+        quantise_wa(0, 0)
+        load_wc(0)
+        quantise_wa(1, 0)
+        load_wc(1)
+        read("a", 0, 0, (1, 2, 3, 4))
+        quantise_wa(0, 1)
+        nc.sync.dma_start(place[:], offs2)
+        weights = placed("weights", 36, [P, S], F32)
+        nc.sync.dma_start(out=weights[:], in_=wgo)
+        quantise_wa(1, 1)
+        late = (5, 6, 0, 2)
+        read("b", 0, 1, (1, 2, 3, 4))
+        read("a", 1, 0, late)
+        round_wc(0, 0)
+        read("a", 0, 1, late)
+        round_wc(0, 1)
+        read_woven(1, 1, late)
+
+        clear(0, 44)
+        subtract(nc.vector, 0, 0, 0, 2048, 52)
+        subtract(nc.gpsimd, 1, 0, 0, SHARE, exps_at["b"][0])
+        scale(0, 0, 60)
+        subtract(nc.vector, 1, 0, SHARE, 2048)
+        subtract(nc.gpsimd, 0, 1, 0, SHARE, exps_at["b"][1])
+        quantise_h(0, 0)
+        scale(1, 0, 64)
+        quantise_wc(0)
+        subtract(nc.vector, 0, 1, SHARE, 2048)
+        subtract(nc.gpsimd, 1, 1, 0, SHARE, exps_at["b"][2])
+        quantise_h(1, 0)
+        scale(0, 1, 138)
+        quantise_h(0, 1)
+        subtract(nc.vector, 1, 1, SHARE, 2048)
+        clear(2, 132)
+        clear(3, 140)
+
+        mix(0, 0, 19)
+        logarithm(0, 0, 160)
+        scatter(0, 0)
+        mix(1, 0, 18)
+        round_wc(1, 0)
+        round_wc(1, 1)
+        logarithm(1, 0, 24)
         quantise_wc(1)
-        clear_beside(2, 77824)
-        mix(0, 1)
-        scatter(0, HALF, S)
-        for i in range(2, 4):
-            mix(i, 0)
-            scatter(i, 0, HALF)
-        for i in range(1, 4):
-            mix(i, 1)
-            scatter(i, HALF, S)
+        weigh(nc.vector, 1, 20)
+        scatter_copy(1)
+        hb[1, 1] = placed("hb11", 24, [P, 4 * HALF], BF16)
+        scale_woven(1, 1, 0, FIRST)
+        mix(2, 0, 30)
+        logarithm(2, 0)
+        weigh(nc.gpsimd, 2, 148)
+        scatter_copy(2)
+        scale_woven(1, 1, FIRST, 2048)
+        mix(3, 0, 150)
+        quantise_h(1, 1)
+        logarithm(3, 0, exps_at["b"][2])
+        scatter(3, 0)
+        for i in range(4):
+            mix(i, 1, 152 + 2 * i)
+            logarithm(i, 1)
+            scatter(i, 1)
+            nc.sync.dma_start(out=rows[i], in_=pages[i][:])

@@ -22,7 +22,6 @@ PASSES = 2
 HALF = S // 2
 KIB = 1024
 SHARE = 768
-FIRST = 768
 
 
 def tile_list_baggage_density_cues_kernel(
@@ -70,7 +69,9 @@ def tile_list_baggage_density_cues_kernel(
         clear_on_one_port(planes[:].rearrange("p a c -> p (a c)").bitcast(I32))
         identity = held("identity", [P, P], F32)
         make_identity(nc, identity[:])
-        clear(1, 124)
+        pages[1] = placed("page1", 124, [P, T2], F32)
+        nc.gpsimd.memset(pages[1][:, 0:1280].bitcast(I32), 0)
+        clear_on_one_port(pages[1][:, 1280:].bitcast(I32))
 
         twords = [placed("twords0", 8, [P, T], U32), placed("twords1", 24, [P, T], U32)]
 
@@ -169,12 +170,12 @@ def tile_list_baggage_density_cues_kernel(
             for t in range(4):
                 nc.sync.dma_start(out=wc_raw[b][:, t, :], in_=rows[t])
 
-        def round_wc(pair, b):
+        def round_wc(pair, b, copy=nc.scalar.copy):
             if b == 0:
                 wc_bf[pair] = placed(f"wc_bf{pair}", 16 + 4 * pair, [P, PASSES, 1024], BF16)
-            nc.scalar.copy(
-                wc_bf[pair][:, b, :].rearrange("p (e q t) -> p q e t", e=2, t=4),
-                wc_raw[b][:].rearrange("p t (q i) -> p q i t", i=4)[:, :, 2 * pair : 2 * pair + 2, :],
+            copy(
+                wc_bf[pair][:, b, :].rearrange("p (e q t) -> p q t e", e=2, t=4),
+                wc_raw[b][:].rearrange("p t (q i) -> p q t i", i=4)[:, :, :, 2 * pair : 2 * pair + 2],
             )
 
         def quantise_wc(pair):
@@ -217,10 +218,10 @@ def tile_list_baggage_density_cues_kernel(
             )
             return exps[reading, b, half]
 
-        def read(reading, b, half, ring):
-            tile = exp_tile(reading, b, half)
-            for t in range(4):
-                bank = take_bank(ring[t])
+        def read(reading, b, half, ring, first=0):
+            tile = exps[reading, b, half] if first else exp_tile(reading, b, half)
+            for t, k in enumerate(ring, first):
+                bank = take_bank(k)
                 multiply(bank[:], reading, b, t, HALF * half, HALF)
                 nc.scalar.activation(tile[:, HALF * t : HALF * (t + 1)], bank[:], ACT.Exp)
 
@@ -243,25 +244,49 @@ def tile_list_baggage_density_cues_kernel(
             views = (difference[b, half], exps["a", b, half], exps["b", b, half])
             engine.tensor_tensor(*[view[:, c0:c1] for view in views], ALU.subtract)
 
-        def scale(b, half, kib):
+        def subtract_first(kib):
+            difference[0, 0] = placed("difference00", kib, [P, 4 * HALF], F32)
+            views = (difference[0, 0], exps["a", 0, 0], exps["b", 0, 0])
+            for j0 in (0, HALF // 2):
+                nc.vector.tensor_tensor(
+                    *[view[:].rearrange("p (t j) -> p t j", t=4)[:, :, j0 : j0 + HALF // 2] for view in views],
+                    ALU.subtract,
+                )
+
+        def scale(b, half, kib, parts=1):
             hb[b, half] = placed(f"hb{b}{half}", kib, [P, 4 * HALF], BF16)
-            nc.vector.tensor_tensor(
-                hb[b, half][:].rearrange("p (c i t) -> p c t i", i=4, t=4),
-                difference[b, half][:].rearrange("p (t c i) -> p c t i", t=4, i=4),
-                gains[:, :, b : b + 1].unsqueeze(1).to_broadcast([P, HALF // 4, 4, 4]),
-                ALU.mult,
-            )
+            fours = HALF // 4 // parts
+            for c0 in range(0, HALF // 4, fours):
+                nc.vector.tensor_tensor(
+                    hb[b, half][:].rearrange("p (c i t) -> p c t i", i=4, t=4)[:, c0 : c0 + fours],
+                    difference[b, half][:].rearrange("p (t c i) -> p c t i", t=4, i=4)[:, c0 : c0 + fours],
+                    gains[:, :, b : b + 1].unsqueeze(1).to_broadcast([P, fours, 4, 4]),
+                    ALU.mult,
+                )
 
-        def scale_woven(b, half, c0, c1):
+        def scale_woven(b, half, part, kib):
+            hb[b, half, part] = placed(f"hb{b}{half}{part}", kib, [P, 4, 256], BF16)
             nc.gpsimd.tensor_tensor(
-                hb[b, half][:, c0:c1].rearrange("p (g c) -> p g c", c=256),
-                difference[b, half][:, c0:c1].rearrange("p (g c) -> p g c", c=256),
-                gain_run[:].rearrange("p j t -> p (j t)").unsqueeze(1).to_broadcast([P, (c1 - c0) // 256, 256]),
+                hb[b, half, part][:],
+                difference[b, half][:, 1024 * part : 1024 * (part + 1)].rearrange("p (g c) -> p g c", c=256),
+                gain_run[:].rearrange("p j t -> p (j t)").unsqueeze(1).to_broadcast([P, 4, 256]),
                 ALU.mult,
             )
 
-        def quantise_h(b, half):
+        def quantise_woven(b, half):
             h_q[b, half] = held(f"h_q{b}{half}", [P, HALF], U32)
+            h_s[b, half] = held(f"h_s{b}{half}", [P, HALF], U8)
+            for part in range(2):
+                cols = slice(256 * part, 256 * (part + 1))
+                nc.vector.quantize_mx(
+                    out=h_q[b, half][:, cols].bitcast(E4M3),
+                    scales=h_s[b, half][:, cols],
+                    in_=hb[b, half, part][:].rearrange("p g c -> p (g c)"),
+                )
+
+        def quantise_h(b, half, kib=None):
+            name = f"h_q{b}{half}"
+            h_q[b, half] = held(name, [P, HALF], U32) if kib is None else placed(name, kib, [P, HALF], U32)
             h_s[b, half] = held(f"h_s{b}{half}", [P, HALF], U8)
             nc.vector.quantize_mx(out=h_q[b, half][:].bitcast(E4M3), scales=h_s[b, half][:], in_=hb[b, half][:])
 
@@ -269,7 +294,7 @@ def tile_list_baggage_density_cues_kernel(
 
         def mix(i, half, kib):
             pair, e = divmod(i, 2)
-            bank = take_bank((1, 3, 4)[len(squares) % 3])
+            bank = take_bank((2, 6, 0)[len(squares) % 3])
             for b in range(PASSES):
                 col = 256 * b + P * e
                 nc.tensor.matmul_mx(
@@ -316,29 +341,30 @@ def tile_list_baggage_density_cues_kernel(
         read("b", 0, 0, (0, 1, 2, 3))
         gather(1, 1, placed("vwords11", 160, [P, HALF], U32))
         load_wa(1, 1)
-        read("b", 1, 0, (4, 5, 6, 0))
+        read("b", 1, 0, (4, 5))
         quantise_wa(0, 0)
         load_wc(0)
         quantise_wa(1, 0)
         load_wc(1)
-        read("a", 0, 0, (1, 2, 3, 4))
+        read("a", 0, 0, (6, 0, 1, 2))
+        read("b", 1, 0, (6, 0), first=2)
         quantise_wa(0, 1)
         nc.sync.dma_start(place[:], offs2)
         weights = placed("weights", 36, [P, S], F32)
         nc.sync.dma_start(out=weights[:], in_=wgo)
         quantise_wa(1, 1)
-        late = (5, 6, 0, 2)
-        read("b", 0, 1, (1, 2, 3, 4))
+        late = (3, 4, 5, 1)
+        read("b", 0, 1, (1, 2, 6, 0))
         read("a", 1, 0, late)
-        round_wc(0, 0)
         read("a", 0, 1, late)
-        round_wc(0, 1)
+        round_wc(0, 0)
         read_woven(1, 1, late)
 
         clear(0, 44)
-        subtract(nc.vector, 0, 0, 0, 2048, 52)
+        subtract_first(52)
         subtract(nc.gpsimd, 1, 0, 0, SHARE, exps_at["b"][0])
-        scale(0, 0, 60)
+        scale(0, 0, 60, parts=2)
+        round_wc(0, 1, nc.vector.tensor_copy)
         subtract(nc.vector, 1, 0, SHARE, 2048)
         subtract(nc.gpsimd, 0, 1, 0, SHARE, exps_at["b"][1])
         quantise_h(0, 0)
@@ -347,31 +373,30 @@ def tile_list_baggage_density_cues_kernel(
         subtract(nc.vector, 0, 1, SHARE, 2048)
         subtract(nc.gpsimd, 1, 1, 0, SHARE, exps_at["b"][2])
         quantise_h(1, 0)
-        scale(0, 1, 138)
-        quantise_h(0, 1)
+        scale(0, 1, 132)
         subtract(nc.vector, 1, 1, SHARE, 2048)
-        clear(2, 132)
-        clear(3, 140)
+        clear(2, exps_at["b"][1] - 4)
+        clear(3, exps_at["b"][1] + 4)
 
         mix(0, 0, 19)
         logarithm(0, 0, 160)
         scatter(0, 0)
-        mix(1, 0, 18)
         round_wc(1, 0)
         round_wc(1, 1)
-        logarithm(1, 0, 24)
+        mix(1, 0, 18)
+        logarithm(1, 0, 25)
         quantise_wc(1)
         weigh(nc.vector, 1, 20)
+        quantise_h(0, 1, 26)
         scatter_copy(1)
-        hb[1, 1] = placed("hb11", 24, [P, 4 * HALF], BF16)
-        scale_woven(1, 1, 0, FIRST)
+        scale_woven(1, 1, 0, 24)
         mix(2, 0, 30)
         logarithm(2, 0)
-        weigh(nc.gpsimd, 2, 148)
+        weigh(nc.vector, 2, 148)
         scatter_copy(2)
-        scale_woven(1, 1, FIRST, 2048)
+        scale_woven(1, 1, 1, 30)
         mix(3, 0, 150)
-        quantise_h(1, 1)
+        quantise_woven(1, 1)
         logarithm(3, 0, exps_at["b"][2])
         scatter(3, 0)
         for i in range(4):

@@ -294,7 +294,7 @@ def tile_list_baggage_density_cues_kernel(
 
         def mix(i, half, kib):
             pair, e = divmod(i, 2)
-            bank = take_bank((2, 6, 0)[len(squares) % 3])
+            bank = take_bank((6, 0, 1)[len(squares) % 3])
             for b in range(PASSES):
                 col = 256 * b + P * e
                 nc.tensor.matmul_mx(
@@ -353,12 +353,15 @@ def tile_list_baggage_density_cues_kernel(
         weights = placed("weights", 36, [P, S], F32)
         nc.sync.dma_start(out=weights[:], in_=wgo)
         quantise_wa(1, 1)
-        late = (3, 4, 5, 1)
-        read("b", 0, 1, (1, 2, 6, 0))
-        read("a", 1, 0, late)
-        read("a", 0, 1, late)
+        read("b", 0, 1, (1,))
+        read("a", 1, 0, (3, 4, 5, 2))
+        read("b", 0, 1, (3,), first=1)
+        read("a", 0, 1, (4, 5))
+        for t in (2, 3):
+            read("b", 0, 1, ((2, 4)[t - 2],), first=t)
+            read("a", 0, 1, ((3, 5)[t - 2],), first=t)
         round_wc(0, 0)
-        read_woven(1, 1, late)
+        read_woven(1, 1, (2, 3, 4, 5))
 
         clear(0, 44)
         subtract_first(52)

@@ -43,15 +43,15 @@ def tile_list_baggage_density_cues_kernel(
             return keep.tile(shape, dtype, name=name, align_bytes=64)
 
         def placed(name, kib, shape, dtype):
-            return arena.tile(shape, dtype, name=name, offset=kib * KIB, align_bytes=64)
+            return arena.tile(shape, dtype, name=name, offset=int(kib * KIB), align_bytes=64)
 
         pick = lists.tile([P, S // 16], U16, name="pick")
         place = lists.tile([P, S // 16], U16, name="place")
 
-        tscale = placed("tscale", 0, [P, T], U8)
-        wbs_raw = held("wbs_raw", [P, H // 4], U32)
+        tscale = placed("tscale", 7, [P, T], U8)
+        wbs_raw = held("wbs_raw", [P, PASSES, H // 4], U32)
         gain_rows = held("gain_rows", [P, 512], F32)
-        planes = held("planes", [P, PASSES, S + H], U8)
+        planes = [held(f"planes{half}", [P, PASSES, HALF], U8) for half in range(2)]
         pages = {}
 
         def clear(i, kib):
@@ -64,16 +64,17 @@ def tile_list_baggage_density_cues_kernel(
             nc.vector.memset(words[:, count // 2 - 1 :], 0)
 
         nc.gpsimd.memset(tscale[:].bitcast(I32), 0)
-        clear_on_one_port(wbs_raw[:].bitcast(I32))
         clear_on_one_port(gain_rows[:].bitcast(I32))
-        clear_on_one_port(planes[:].rearrange("p a c -> p (a c)").bitcast(I32))
+        clear_on_one_port(wbs_raw[:].rearrange("p a c -> p (a c)").bitcast(I32))
+        for plane in planes:
+            clear_on_one_port(plane[:].rearrange("p a c -> p (a c)").bitcast(I32))
         identity = held("identity", [P, P], F32)
         make_identity(nc, identity[:])
         pages[1] = placed("page1", 124, [P, T2], F32)
         nc.gpsimd.memset(pages[1][:, 0:1280].bitcast(I32), 0)
         clear_on_one_port(pages[1][:, 1280:].bitcast(I32))
 
-        twords = [placed("twords0", 8, [P, T], U32), placed("twords1", 24, [P, T], U32)]
+        twords = [placed("twords0", 140, [P, T], U32), placed("twords1", 24, [P, T], U32)]
 
         def load_table(a, c0=0, c1=T):
             nc.sync.dma_start(
@@ -86,31 +87,19 @@ def tile_list_baggage_density_cues_kernel(
         nc.sync.dma_start(
             out=tscale[0:P:4, :].bitcast(I32), in_=tab_scales.bitcast(I32).rearrange("a q t -> q a t")
         )
-        nc.sync.dma_start(
-            out=wbs_raw[0:P:4, :].bitcast(I32), in_=wb_scales.bitcast(I32).rearrange("a q c -> q a c")
-        )
-        nc.sync.dma_start(out=gain_rows[0:PASSES, :], in_=gain.rearrange("(b c) -> b c", b=PASSES))
         load_table(0, T // 4, T)
-        wbw_raw = placed("wbw_raw", 16, [P, PASSES * H // 2], U32)
+        wbw_raw = placed("wbw_raw", 163.5, [P, PASSES * H // 2], U32)
         nc.sync.dma_start(
             out=wbw_raw[:].bitcast(I32).rearrange("p (a c) -> p a c", a=PASSES),
             in_=wb_words.bitcast(I32).rearrange("a p c -> p a c"),
         )
-        load_table(1)
-
-        rows_in = held("rows_in", [P, (S + H) // 4], U32)
-        nc.scalar.copy(
-            rows_in[:, S // 4 :].rearrange("p (t m) -> p t m", t=4),
-            wbs_raw[:].rearrange("p (m t) -> p t m", t=4),
-        )
-        gscale = placed("gscale", 2, [P, S], U8)
-        nc.vector.tensor_copy(gscale[:], tscale[:].indirect(pick[:]))
-        nc.vector.tensor_copy(rows_in[:, 0 : S // 4], gscale[:].bitcast(U32))
+        nc.sync.dma_start(out=gain_rows[0:PASSES, :], in_=gain.rearrange("(b c) -> b c", b=PASSES))
         for d in range(4):
             nc.sync.dma_start(
-                out=planes[32 * d : 32 * d + 4, :, :].rearrange("p a c -> p (a c)").bitcast(I32),
-                in_=rows_in[32 * d : 32 * (d + 1) : 4, :].bitcast(I32),
+                out=wbs_raw[32 * d : 32 * d + 4, :, :].bitcast(I32),
+                in_=wb_scales.bitcast(I32)[:, 4 * d : 4 * d + 4, :].rearrange("a r c -> r a c"),
             )
+        load_table(1)
 
         wbw = held("wbw", [P, PASSES * H // 2], U32)
         wbw_bytes = wbw[:].bitcast(U8)
@@ -119,22 +108,39 @@ def tile_list_baggage_density_cues_kernel(
             wbw_raw[:].rearrange("p (a m t u) -> p a t m u", a=PASSES, t=4, u=2),
         )
 
+        wb_planes = placed("wb_planes", 162, [P, PASSES, H // 4], U32)
+        nc.scalar.copy(
+            wb_planes[:].rearrange("p a (t m) -> p a t m", t=4),
+            wbs_raw[:].rearrange("p a (m t) -> p a t m", t=4),
+        )
         gains = banks.tile([P, 4, P], F32, name="gains", offset=2048 * 7)
-        gain_dealt = held("gain_dealt", [P, 512], F32)
-        nc.scalar.activation(
+        gain_dealt = placed("gain_dealt", 164, [P, 512], F32)
+        nc.scalar.copy(
             gain_dealt[:].rearrange("p (t m u) -> p t m u", t=4, u=4),
             gain_rows[:].rearrange("p (m t u) -> p t m u", t=4, u=4),
-            ACT.Copy,
         )
         for t in range(4):
             nc.tensor.transpose(gains[:, t, :], gain_dealt[:, P * t : P * (t + 1)], identity[:])
         gain_run = held("gain_run", [P, 64, 4], F32)
         nc.scalar.copy(gain_run[:], gains[:, :, 1:2].rearrange("p t o -> p o t").to_broadcast([P, 64, 4]))
 
+        gscale = [held(f"gscale{half}", [P, HALF], U8) for half in range(2)]
+
+        def move_planes(half):
+            for d in range(4):
+                nc.sync.dma_start(
+                    out=planes[half][32 * d : 32 * d + 4, :, :].rearrange("p a c -> p (a c)").bitcast(I32),
+                    in_=gscale[half][32 * d : 32 * (d + 1) : 4, :].bitcast(I32),
+                )
+
+        for half in range(2):
+            nc.vector.tensor_copy(gscale[half][:], tscale[:].indirect(pick[:, 32 * half : 32 * (half + 1)]))
+        move_planes(0)
+
         wa_raw, wa_q, wa_s = {}, {}, {}
 
         def load_wa(a, b):
-            wa_raw[a, b] = placed(f"wa_raw{a}{b}", 8 * (a + 2 * b), [P, 4, 512], F32)
+            wa_raw[a, b] = placed(f"wa_raw{a}{b}", (0, 8, 166, 24)[a + 2 * b], [P, 4, 512], F32)
             nc.sync.dma_start(
                 out=wa_raw[a, b][:],
                 in_=wa[512 * a : 512 * (a + 1), 512 * b : 512 * (b + 1)].rearrange("(p i) c -> p i c", i=4),
@@ -193,7 +199,7 @@ def tile_list_baggage_density_cues_kernel(
                 return wa_q[a, b][:, cols].bitcast(E4M3), wa_s[a, b][:, cols]
             col = t * 256 + b * P
             codes = wbw_bytes[:, 2 * (a * H + col) : 2 * (a * H + col + P)]
-            return codes.bitcast(E2M1), planes[:, a, S + col : S + col + P]
+            return codes.bitcast(E2M1), wb_planes[:].bitcast(U8)[:, a, col : col + P]
 
         def multiply(bank, reading, b, t, j0, width):
             half, c0 = divmod(j0, HALF)
@@ -204,7 +210,7 @@ def tile_list_baggage_density_cues_kernel(
                     lhsT=codes,
                     lhsT_scale=scales,
                     rhs=vwords[a, half][:, c0 : c0 + width].bitcast(E4M3),
-                    rhs_scale=planes[:, a, j0 : j0 + width],
+                    rhs_scale=planes[half][:, a, c0 : c0 + width],
                     start=(a == 0),
                     stop=(a == PASSES - 1),
                 )
@@ -333,9 +339,10 @@ def tile_list_baggage_density_cues_kernel(
             nc.vector.tensor_copy(slots(i, 0), weighted[i][:])
 
         load_wa(0, 0)
+        load_wa(1, 0)
+        move_planes(1)
         gather(0, 0, held("vwords00", [P, HALF], U32))
         gather(0, 1, held("vwords01", [P, HALF], U32))
-        load_wa(1, 0)
         load_wa(0, 1)
         gather(1, 0, held("vwords10", [P, HALF], U32))
         read("b", 0, 0, (0, 1, 2, 3))

@@ -176,10 +176,10 @@ def tile_list_baggage_density_cues_kernel(
             for t in range(4):
                 nc.sync.dma_start(out=wc_raw[b][:, t, :], in_=rows[t])
 
-        def round_wc(pair, b, copy=nc.scalar.copy):
+        def round_wc(pair, b):
             if b == 0:
-                wc_bf[pair] = placed(f"wc_bf{pair}", 16 + 4 * pair, [P, PASSES, 1024], BF16)
-            copy(
+                wc_bf[pair] = placed(f"wc_bf{pair}", (108, 20)[pair], [P, PASSES, 1024], BF16)
+            nc.scalar.copy(
                 wc_bf[pair][:, b, :].rearrange("p (e q t) -> p q t e", e=2, t=4),
                 wc_raw[b][:].rearrange("p t (q i) -> p q t i", i=4)[:, :, :, 2 * pair : 2 * pair + 2],
             )
@@ -216,7 +216,7 @@ def tile_list_baggage_density_cues_kernel(
                 )
 
         exps, difference, hb, h_q, h_s = {}, {}, {}, {}, {}
-        exps_at = {"a": (60, 76, 92, 108), "b": (68, 84, 100, 116)}
+        exps_at = {"a": (60, 76, 92, 132), "b": (68, 84, 100, 116)}
 
         def exp_tile(reading, b, half):
             exps[reading, b, half] = placed(
@@ -300,7 +300,7 @@ def tile_list_baggage_density_cues_kernel(
 
         def mix(i, half, kib):
             pair, e = divmod(i, 2)
-            bank = take_bank((6, 0, 1)[len(squares) % 3])
+            bank = take_bank((5, 6, 0)[len(squares) % 3])
             for b in range(PASSES):
                 col = 256 * b + P * e
                 nc.tensor.matmul_mx(
@@ -348,42 +348,38 @@ def tile_list_baggage_density_cues_kernel(
         read("b", 0, 0, (0, 1, 2, 3))
         gather(1, 1, placed("vwords11", 160, [P, HALF], U32))
         load_wa(1, 1)
-        read("b", 1, 0, (4, 5))
+        read("b", 1, 0, (0, 1, 2, 3))
         quantise_wa(0, 0)
         load_wc(0)
         quantise_wa(1, 0)
         load_wc(1)
-        read("a", 0, 0, (6, 0, 1, 2))
-        read("b", 1, 0, (6, 0), first=2)
+        read("a", 0, 0, (4, 5, 6, 0))
         quantise_wa(0, 1)
         nc.sync.dma_start(place[:], offs2)
         weights = placed("weights", 36, [P, S], F32)
         nc.sync.dma_start(out=weights[:], in_=wgo)
         quantise_wa(1, 1)
-        read("b", 0, 1, (1,))
-        read("a", 1, 0, (3, 4, 5, 2))
-        read("b", 0, 1, (3,), first=1)
-        read("a", 0, 1, (4, 5))
-        for t in (2, 3):
-            read("b", 0, 1, ((2, 4)[t - 2],), first=t)
-            read("a", 0, 1, ((3, 5)[t - 2],), first=t)
+        late = (1, 2, 3, 4)
+        read("b", 0, 1, (4, 5, 6, 0))
+        read("a", 1, 0, late)
         round_wc(0, 0)
-        read_woven(1, 1, (2, 3, 4, 5))
+        read("a", 0, 1, late)
+        round_wc(0, 1)
+        read_woven(1, 1, late)
 
         clear(0, 44)
         subtract_first(52)
         subtract(nc.gpsimd, 1, 0, 0, SHARE, exps_at["b"][0])
         scale(0, 0, 60, parts=2)
-        round_wc(0, 1, nc.vector.tensor_copy)
         subtract(nc.vector, 1, 0, SHARE, 2048)
         subtract(nc.gpsimd, 0, 1, 0, SHARE, exps_at["b"][1])
         quantise_h(0, 0)
         scale(1, 0, 64)
-        quantise_wc(0)
         subtract(nc.vector, 0, 1, SHARE, 2048)
-        subtract(nc.gpsimd, 1, 1, 0, SHARE, exps_at["b"][2])
+        quantise_wc(0)
+        subtract(nc.gpsimd, 1, 1, 0, SHARE, 104)
         quantise_h(1, 0)
-        scale(0, 1, 132)
+        scale(0, 1, 140)
         subtract(nc.vector, 1, 1, SHARE, 2048)
         clear(2, exps_at["b"][1] - 4)
         clear(3, exps_at["b"][1] + 4)
@@ -407,7 +403,7 @@ def tile_list_baggage_density_cues_kernel(
         scale_woven(1, 1, 1, 30)
         mix(3, 0, 150)
         quantise_woven(1, 1)
-        logarithm(3, 0, exps_at["b"][2])
+        logarithm(3, 0, 104)
         scatter(3, 0)
         for i in range(4):
             mix(i, 1, 152 + 2 * i)

@@ -22,6 +22,7 @@ PASSES = 2
 HALF = S // 2
 KIB = 1024
 SHARE = 768
+SHARE_BEHIND_QUANTISE = 896
 
 
 def tile_list_baggage_density_cues_kernel(
@@ -88,11 +89,23 @@ def tile_list_baggage_density_cues_kernel(
             out=tscale[0:P:4, :].bitcast(I32), in_=tab_scales.bitcast(I32).rearrange("a q t -> q a t")
         )
         load_table(0, T // 4, T)
-        wbw_raw = placed("wbw_raw", 163.5, [P, PASSES * H // 2], U32)
-        nc.sync.dma_start(
-            out=wbw_raw[:].bitcast(I32).rearrange("p (a c) -> p a c", a=PASSES),
-            in_=wb_words.bitcast(I32).rearrange("a p c -> p a c"),
-        )
+        wbw_raw, wbw = {}, {}
+
+        def load_wb(b, kib):
+            wbw_raw[b] = placed(f"wbw_raw{b}", kib, [P, PASSES, 256], U32)
+            nc.sync.dma_start(
+                out=wbw_raw[b][:].bitcast(I32),
+                in_=wb_words.bitcast(I32)[:, :, 256 * b : 256 * (b + 1)].rearrange("a p c -> p a c"),
+            )
+
+        def order_wb(b):
+            wbw[b] = held(f"wbw{b}", [P, PASSES, 256], U32)
+            nc.scalar.copy(
+                wbw[b][:].rearrange("p a (t m u) -> p a t m u", t=4, u=2),
+                wbw_raw[b][:].rearrange("p a (m t u) -> p a t m u", t=4, u=2),
+            )
+
+        load_wb(0, 163)
         nc.sync.dma_start(out=gain_rows[0:PASSES, :], in_=gain.rearrange("(b c) -> b c", b=PASSES))
         for d in range(4):
             nc.sync.dma_start(
@@ -100,14 +113,9 @@ def tile_list_baggage_density_cues_kernel(
                 in_=wb_scales.bitcast(I32)[:, 4 * d : 4 * d + 4, :].rearrange("a r c -> r a c"),
             )
         load_table(1)
+        load_wb(1, 166)
 
-        wbw = held("wbw", [P, PASSES * H // 2], U32)
-        wbw_bytes = wbw[:].bitcast(U8)
-        nc.scalar.copy(
-            wbw[:].rearrange("p (a t m u) -> p a t m u", a=PASSES, t=4, u=2),
-            wbw_raw[:].rearrange("p (a m t u) -> p a t m u", a=PASSES, t=4, u=2),
-        )
-
+        order_wb(0)
         wb_planes = placed("wb_planes", 162, [P, PASSES, H // 4], U32)
         nc.scalar.copy(
             wb_planes[:].rearrange("p a (t m) -> p a t m", t=4),
@@ -121,6 +129,7 @@ def tile_list_baggage_density_cues_kernel(
         )
         for t in range(4):
             nc.tensor.transpose(gains[:, t, :], gain_dealt[:, P * t : P * (t + 1)], identity[:])
+        order_wb(1)
         gain_run = held("gain_run", [P, 64, 4], F32)
         nc.scalar.copy(gain_run[:], gains[:, :, 1:2].rearrange("p t o -> p o t").to_broadcast([P, 64, 4]))
 
@@ -198,7 +207,7 @@ def tile_list_baggage_density_cues_kernel(
                 cols = slice(P * t, P * (t + 1))
                 return wa_q[a, b][:, cols].bitcast(E4M3), wa_s[a, b][:, cols]
             col = t * 256 + b * P
-            codes = wbw_bytes[:, 2 * (a * H + col) : 2 * (a * H + col + P)]
+            codes = wbw[b][:].bitcast(U8)[:, a, 2 * P * t : 2 * P * (t + 1)]
             return codes.bitcast(E2M1), wb_planes[:].bitcast(U8)[:, a, col : col + P]
 
         def multiply(bank, reading, b, t, j0, width):
@@ -300,7 +309,7 @@ def tile_list_baggage_density_cues_kernel(
 
         def mix(i, half, kib):
             pair, e = divmod(i, 2)
-            bank = take_bank((5, 6, 0)[len(squares) % 3])
+            bank = take_bank((4, 5, 6)[len(squares) % 3])
             for b in range(PASSES):
                 col = 256 * b + P * e
                 nc.tensor.matmul_mx(
@@ -353,14 +362,15 @@ def tile_list_baggage_density_cues_kernel(
         load_wc(0)
         quantise_wa(1, 0)
         load_wc(1)
-        read("a", 0, 0, (4, 5, 6, 0))
+        read("b", 0, 1, (0,))
+        read("a", 0, 0, (4, 5, 6, 1))
         quantise_wa(0, 1)
         nc.sync.dma_start(place[:], offs2)
         weights = placed("weights", 36, [P, S], F32)
         nc.sync.dma_start(out=weights[:], in_=wgo)
         quantise_wa(1, 1)
-        late = (1, 2, 3, 4)
-        read("b", 0, 1, (4, 5, 6, 0))
+        late = (2, 3, 0, 1)
+        read("b", 0, 1, (4, 5, 6), first=1)
         read("a", 1, 0, late)
         round_wc(0, 0)
         read("a", 0, 1, late)
@@ -372,15 +382,15 @@ def tile_list_baggage_density_cues_kernel(
         subtract(nc.gpsimd, 1, 0, 0, SHARE, exps_at["b"][0])
         scale(0, 0, 60, parts=2)
         subtract(nc.vector, 1, 0, SHARE, 2048)
-        subtract(nc.gpsimd, 0, 1, 0, SHARE, exps_at["b"][1])
+        subtract(nc.gpsimd, 0, 1, 0, SHARE_BEHIND_QUANTISE, exps_at["b"][1])
         quantise_h(0, 0)
         scale(1, 0, 64)
-        subtract(nc.vector, 0, 1, SHARE, 2048)
+        subtract(nc.vector, 0, 1, SHARE_BEHIND_QUANTISE, 2048)
         quantise_wc(0)
-        subtract(nc.gpsimd, 1, 1, 0, SHARE, 104)
+        subtract(nc.gpsimd, 1, 1, 0, SHARE_BEHIND_QUANTISE, 104)
         quantise_h(1, 0)
         scale(0, 1, 140)
-        subtract(nc.vector, 1, 1, SHARE, 2048)
+        subtract(nc.vector, 1, 1, SHARE_BEHIND_QUANTISE, 2048)
         clear(2, exps_at["b"][1] - 4)
         clear(3, exps_at["b"][1] + 4)
 

@@ -130,8 +130,8 @@ def tile_list_baggage_density_cues_kernel(
         for t in range(4):
             nc.tensor.transpose(gains[:, t, :], gain_dealt[:, P * t : P * (t + 1)], identity[:])
         order_wb(1)
-        gain_run = held("gain_run", [P, 64, 4], F32)
-        nc.scalar.copy(gain_run[:], gains[:, :, 1:2].rearrange("p t o -> p o t").to_broadcast([P, 64, 4]))
+        last_gains = held("last_gains", [P, 4], F32)
+        nc.scalar.copy(last_gains[:], gains[:, :, 1:2].rearrange("p t o -> p (t o)"))
 
         gscale = [held(f"gscale{half}", [P, HALF], U8) for half in range(2)]
 
@@ -187,7 +187,7 @@ def tile_list_baggage_density_cues_kernel(
 
         def round_wc(pair, b):
             if b == 0:
-                wc_bf[pair] = placed(f"wc_bf{pair}", (108, 20)[pair], [P, PASSES, 1024], BF16)
+                wc_bf[pair] = placed(f"wc_bf{pair}", (108, 151)[pair], [P, PASSES, 1024], BF16)
             nc.scalar.copy(
                 wc_bf[pair][:, b, :].rearrange("p (e q t) -> p q t e", e=2, t=4),
                 wc_raw[b][:].rearrange("p t (q i) -> p q t i", i=4)[:, :, :, 2 * pair : 2 * pair + 2],
@@ -195,7 +195,7 @@ def tile_list_baggage_density_cues_kernel(
 
         def quantise_wc(pair):
             wc_q[pair] = held(f"wc_q{pair}", [P, 512], U32)
-            wc_s[pair] = held(f"wc_s{pair}", [P, 512], U8)
+            wc_s[pair] = placed(f"wc_s{pair}", (144, 140)[pair], [P, 512], U8)
             nc.vector.quantize_mx(
                 out=wc_q[pair][:].bitcast(E4M3),
                 scales=wc_s[pair][:],
@@ -240,19 +240,6 @@ def tile_list_baggage_density_cues_kernel(
                 multiply(bank[:], reading, b, t, HALF * half, HALF)
                 nc.scalar.activation(tile[:, HALF * t : HALF * (t + 1)], bank[:], ACT.Exp)
 
-        def read_woven(b, half, ring):
-            tiles = {reading: exp_tile(reading, b, half) for reading in "ba"}
-            for c in range(4):
-                for k, reading in enumerate("ba"):
-                    bank = take_bank(ring[(2 * c + k) % len(ring)])
-                    for t in range(4):
-                        multiply(bank[:, P * t : P * (t + 1)], reading, b, t, HALF * half + P * c, P)
-                    nc.scalar.activation(
-                        tiles[reading][:, HALF * c : HALF * (c + 1)].rearrange("p (j t) -> p j t", t=4),
-                        bank[:].rearrange("p (t j) -> p j t", t=4),
-                        ACT.Exp,
-                    )
-
         def subtract(engine, b, half, c0, c1, kib=None):
             if kib is not None:
                 difference[b, half] = placed(f"difference{b}{half}", kib, [P, 4 * HALF], F32)
@@ -279,29 +266,30 @@ def tile_list_baggage_density_cues_kernel(
                     ALU.mult,
                 )
 
-        def scale_woven(b, half, part, kib):
-            hb[b, half, part] = placed(f"hb{b}{half}{part}", kib, [P, 4, 256], BF16)
+        def subtract_last(c0, c1, kib):
+            difference[1, 1, c0] = placed(f"difference11_{c0}", kib, [P, c1 - c0], F32)
             nc.gpsimd.tensor_tensor(
-                hb[b, half, part][:],
-                difference[b, half][:, 1024 * part : 1024 * (part + 1)].rearrange("p (g c) -> p g c", c=256),
-                gain_run[:].rearrange("p j t -> p (j t)").unsqueeze(1).to_broadcast([P, 4, 256]),
-                ALU.mult,
+                difference[1, 1, c0][:], exps["a", 1, 1][:, c0:c1], exps["b", 1, 1][:, c0:c1], ALU.subtract
             )
 
-        def quantise_woven(b, half):
-            h_q[b, half] = held(f"h_q{b}{half}", [P, HALF], U32)
-            h_s[b, half] = held(f"h_s{b}{half}", [P, HALF], U8)
-            for part in range(2):
-                cols = slice(256 * part, 256 * (part + 1))
-                nc.vector.quantize_mx(
-                    out=h_q[b, half][:, cols].bitcast(E4M3),
-                    scales=h_s[b, half][:, cols],
-                    in_=hb[b, half, part][:].rearrange("p g c -> p (g c)"),
-                )
+        def scale_last(start, c0, c1):
+            t = c0 // HALF
+            nc.scalar.activation(
+                scaled[:, c0:c1],
+                difference[1, 1, start][:, c0 - start : c1 - start],
+                ACT.Copy,
+                scale=last_gains[:, t : t + 1],
+            )
 
-        def quantise_h(b, half, kib=None):
-            name = f"h_q{b}{half}"
-            h_q[b, half] = held(name, [P, HALF], U32) if kib is None else placed(name, kib, [P, HALF], U32)
+        def weave(kib):
+            hb[1, 1] = placed("hb11", kib, [P, 4 * HALF], BF16)
+            nc.scalar.copy(
+                hb[1, 1][:].rearrange("p (c i t) -> p c t i", i=4, t=4),
+                scaled[:].rearrange("p (t c i) -> p c t i", t=4, i=4),
+            )
+
+        def quantise_h(b, half):
+            h_q[b, half] = held(f"h_q{b}{half}", [P, HALF], U32)
             h_s[b, half] = held(f"h_s{b}{half}", [P, HALF], U8)
             nc.vector.quantize_mx(out=h_q[b, half][:].bitcast(E4M3), scales=h_s[b, half][:], in_=hb[b, half][:])
 
@@ -324,9 +312,9 @@ def tile_list_baggage_density_cues_kernel(
             squares[i, half] = placed(f"square{i}{half}", kib, [P, HALF], F32)
             nc.scalar.activation(squares[i, half][:], bank[:], ACT.Square)
 
-        def logarithm(i, half, kib=None):
-            ys[i, half] = squares[i, half] if kib is None else placed(f"y{i}{half}", kib, [P, HALF], F32)
-            nc.scalar.activation(ys[i, half][:], squares[i, half][:], ACT.Ln, bias=1.0)
+        def logarithm(i, half, into=None):
+            ys[i, half] = squares[i, half][:] if into is None else into
+            nc.scalar.activation(ys[i, half], squares[i, half][:], ACT.Ln, bias=1.0)
 
         rows = out.rearrange("(p i) t -> i p t", i=4)
 
@@ -335,17 +323,8 @@ def tile_list_baggage_density_cues_kernel(
 
         def scatter(i, half):
             nc.vector.tensor_tensor(
-                slots(i, half), ys[i, half][:], weights[:, HALF * half : HALF * (half + 1)], ALU.mult
+                slots(i, half), ys[i, half], weights[:, HALF * half : HALF * (half + 1)], ALU.mult
             )
-
-        weighted = {}
-
-        def weigh(engine, i, kib):
-            weighted[i] = placed(f"weighted{i}", kib, [P, HALF], F32)
-            engine.tensor_tensor(weighted[i][:], ys[i, 0][:], weights[:, 0:HALF], ALU.mult)
-
-        def scatter_copy(i):
-            nc.vector.tensor_copy(slots(i, 0), weighted[i][:])
 
         load_wa(0, 0)
         load_wa(1, 0)
@@ -355,7 +334,7 @@ def tile_list_baggage_density_cues_kernel(
         load_wa(0, 1)
         gather(1, 0, held("vwords10", [P, HALF], U32))
         read("b", 0, 0, (0, 1, 2, 3))
-        gather(1, 1, placed("vwords11", 160, [P, HALF], U32))
+        gather(1, 1, placed("vwords11", 174, [P, HALF], U32))
         load_wa(1, 1)
         read("b", 1, 0, (0, 1, 2, 3))
         quantise_wa(0, 0)
@@ -375,7 +354,9 @@ def tile_list_baggage_density_cues_kernel(
         round_wc(0, 0)
         read("a", 0, 1, late)
         round_wc(0, 1)
-        read_woven(1, 1, late)
+        for t in range(4):
+            read("b", 1, 1, (late[2 * t % 4],), first=t)
+            read("a", 1, 1, (late[(2 * t + 1) % 4],), first=t)
 
         clear(0, 44)
         subtract_first(52)
@@ -385,38 +366,40 @@ def tile_list_baggage_density_cues_kernel(
         subtract(nc.gpsimd, 0, 1, 0, SHARE_BEHIND_QUANTISE, exps_at["b"][1])
         quantise_h(0, 0)
         scale(1, 0, 64)
-        subtract(nc.vector, 0, 1, SHARE_BEHIND_QUANTISE, 2048)
         quantise_wc(0)
-        subtract(nc.gpsimd, 1, 1, 0, SHARE_BEHIND_QUANTISE, 104)
         quantise_h(1, 0)
+        subtract(nc.vector, 0, 1, SHARE_BEHIND_QUANTISE, 2048)
+        subtract_last(0, SHARE, 104)
         scale(0, 1, 140)
-        subtract(nc.vector, 1, 1, SHARE_BEHIND_QUANTISE, 2048)
-        clear(2, exps_at["b"][1] - 4)
-        clear(3, exps_at["b"][1] + 4)
+        quantise_h(0, 1)
 
-        mix(0, 0, 19)
-        logarithm(0, 0, 160)
-        scatter(0, 0)
+        mix(0, 0, 150)
+        logarithm(0, 0, placed("y00", 174, [P, HALF], F32)[:])
+        weighted = placed("weighted", 140, [P, HALF], F32)
+        nc.vector.tensor_tensor(weighted[:], ys[0, 0], weights[:, 0:HALF], ALU.mult)
+        nc.vector.tensor_copy(slots(0, 0), weighted[:])
+        subtract_last(SHARE, 4 * HALF, 172)
         round_wc(1, 0)
         round_wc(1, 1)
-        mix(1, 0, 18)
-        logarithm(1, 0, 25)
+        mix(1, 0, 149)
+        logarithm(1, 0, placed("y10", 16, [P, HALF], F32)[:])
         quantise_wc(1)
-        weigh(nc.vector, 1, 20)
-        quantise_h(0, 1, 26)
-        scatter_copy(1)
-        scale_woven(1, 1, 0, 24)
-        mix(2, 0, 30)
-        logarithm(2, 0)
-        weigh(nc.vector, 2, 148)
-        scatter_copy(2)
-        scale_woven(1, 1, 1, 30)
-        mix(3, 0, 150)
-        quantise_woven(1, 1)
-        logarithm(3, 0, 104)
+        clear(2, 145)
+        clear(3, 153)
+        scatter(1, 0)
+        scaled = placed("scaled", 108, [P, 4 * HALF], F32)
+        for start, c0, c1 in ((0, 0, HALF), (0, HALF, SHARE), (SHARE, SHARE, 2 * HALF), (SHARE, 2 * HALF, 3 * HALF), (SHARE, 3 * HALF, 4 * HALF)):
+            scale_last(start, c0, c1)
+        mix(2, 0, 172)
+        logarithm(2, 0, placed("y20", 26, [P, HALF], F32)[:])
+        scatter(2, 0)
+        weave(169)
+        quantise_h(1, 1)
+        mix(3, 0, 108)
+        logarithm(3, 0)
         scatter(3, 0)
         for i in range(4):
-            mix(i, 1, 152 + 2 * i)
+            mix(i, 1, 68 + 2 * i)
             logarithm(i, 1)
             scatter(i, 1)
             nc.sync.dma_start(out=rows[i], in_=pages[i][:])

@@ -22,6 +22,7 @@ PASSES = 2
 HALF = S // 2
 KIB = 1024
 SHARE = 768
+LAST_SHARE = 832
 SHARE_BEHIND_QUANTISE = 896
 
 
@@ -185,17 +186,17 @@ def tile_list_baggage_density_cues_kernel(
             for t in range(4):
                 nc.sync.dma_start(out=wc_raw[b][:, t, :], in_=rows[t])
 
-        def round_wc(pair, b):
+        def round_wc(pair, b, copy=nc.scalar.copy, q0=0, q1=P):
             if b == 0:
                 wc_bf[pair] = placed(f"wc_bf{pair}", (108, 151)[pair], [P, PASSES, 1024], BF16)
-            nc.scalar.copy(
-                wc_bf[pair][:, b, :].rearrange("p (e q t) -> p q t e", e=2, t=4),
-                wc_raw[b][:].rearrange("p t (q i) -> p q t i", i=4)[:, :, :, 2 * pair : 2 * pair + 2],
+            copy(
+                wc_bf[pair][:, b, :].rearrange("p (e q t) -> p q t e", e=2, t=4)[:, q0:q1],
+                wc_raw[b][:].rearrange("p t (q i) -> p q t i", i=4)[:, q0:q1, :, 2 * pair : 2 * pair + 2],
             )
 
         def quantise_wc(pair):
             wc_q[pair] = held(f"wc_q{pair}", [P, 512], U32)
-            wc_s[pair] = placed(f"wc_s{pair}", (144, 140)[pair], [P, 512], U8)
+            wc_s[pair] = placed(f"wc_s{pair}", (144, 18)[pair], [P, 512], U8)
             nc.vector.quantize_mx(
                 out=wc_q[pair][:].bitcast(E4M3),
                 scales=wc_s[pair][:],
@@ -288,9 +289,10 @@ def tile_list_baggage_density_cues_kernel(
                 scaled[:].rearrange("p (t c i) -> p c t i", t=4, i=4),
             )
 
-        def quantise_h(b, half):
+        def quantise_h(b, half, kib=None):
             h_q[b, half] = held(f"h_q{b}{half}", [P, HALF], U32)
-            h_s[b, half] = held(f"h_s{b}{half}", [P, HALF], U8)
+            name = f"h_s{b}{half}"
+            h_s[b, half] = held(name, [P, HALF], U8) if kib is None else placed(name, kib, [P, HALF], U8)
             nc.vector.quantize_mx(out=h_q[b, half][:].bitcast(E4M3), scales=h_s[b, half][:], in_=hb[b, half][:])
 
         squares, ys = {}, {}
@@ -353,7 +355,7 @@ def tile_list_baggage_density_cues_kernel(
         read("a", 1, 0, late)
         round_wc(0, 0)
         read("a", 0, 1, late)
-        round_wc(0, 1)
+        round_wc(0, 1, q0=P // 2)
         for t in range(4):
             read("b", 1, 1, (late[2 * t % 4],), first=t)
             read("a", 1, 1, (late[(2 * t + 1) % 4],), first=t)
@@ -362,6 +364,7 @@ def tile_list_baggage_density_cues_kernel(
         subtract_first(52)
         subtract(nc.gpsimd, 1, 0, 0, SHARE, exps_at["b"][0])
         scale(0, 0, 60, parts=2)
+        round_wc(0, 1, nc.vector.tensor_copy, 0, P // 2)
         subtract(nc.vector, 1, 0, SHARE, 2048)
         subtract(nc.gpsimd, 0, 1, 0, SHARE_BEHIND_QUANTISE, exps_at["b"][1])
         quantise_h(0, 0)
@@ -369,16 +372,19 @@ def tile_list_baggage_density_cues_kernel(
         quantise_wc(0)
         quantise_h(1, 0)
         subtract(nc.vector, 0, 1, SHARE_BEHIND_QUANTISE, 2048)
-        subtract_last(0, SHARE, 104)
+        subtract_last(0, LAST_SHARE, 104)
         scale(0, 1, 140)
-        quantise_h(0, 1)
 
         mix(0, 0, 150)
-        logarithm(0, 0, placed("y00", 174, [P, HALF], F32)[:])
-        weighted = placed("weighted", 140, [P, HALF], F32)
-        nc.vector.tensor_tensor(weighted[:], ys[0, 0], weights[:, 0:HALF], ALU.mult)
+        first_y = placed("y00", 174, [P, HALF], F32)
+        weighted = placed("weighted", 18, [P, HALF], F32)
+        for j0 in (0, HALF // 2):
+            cols = slice(j0, j0 + HALF // 2)
+            nc.scalar.activation(first_y[:, cols], squares[0, 0][:, cols], ACT.Ln, bias=1.0)
+            nc.vector.tensor_tensor(weighted[:, cols], first_y[:, cols], weights[:, cols], ALU.mult)
+        quantise_h(0, 1, 175)
         nc.vector.tensor_copy(slots(0, 0), weighted[:])
-        subtract_last(SHARE, 4 * HALF, 172)
+        subtract_last(LAST_SHARE, 4 * HALF, 170)
         round_wc(1, 0)
         round_wc(1, 1)
         mix(1, 0, 149)
@@ -388,12 +394,12 @@ def tile_list_baggage_density_cues_kernel(
         clear(3, 153)
         scatter(1, 0)
         scaled = placed("scaled", 108, [P, 4 * HALF], F32)
-        for start, c0, c1 in ((0, 0, HALF), (0, HALF, SHARE), (SHARE, SHARE, 2 * HALF), (SHARE, 2 * HALF, 3 * HALF), (SHARE, 3 * HALF, 4 * HALF)):
+        for start, c0, c1 in ((0, 0, HALF), (0, HALF, LAST_SHARE), (LAST_SHARE, LAST_SHARE, 2 * HALF), (LAST_SHARE, 2 * HALF, 3 * HALF), (LAST_SHARE, 3 * HALF, 4 * HALF)):
             scale_last(start, c0, c1)
-        mix(2, 0, 172)
+        mix(2, 0, 170)
         logarithm(2, 0, placed("y20", 26, [P, HALF], F32)[:])
         scatter(2, 0)
-        weave(169)
+        weave(167)
         quantise_h(1, 1)
         mix(3, 0, 108)
         logarithm(3, 0)

from contextlib import ExitStack

import concourse.mybir as mybir
from concourse.masks import make_identity

K, H, N, T, S, T2 = 1024, 1024, 512, 2048, 1024, 2048
FLOPS = 2 * (2 * K * H * S + H * N * S)

F32 = mybir.dt.float32
BF16 = mybir.dt.bfloat16
I32 = mybir.dt.int32
U32 = mybir.dt.uint32
U16 = mybir.dt.uint16
U8 = mybir.dt.uint8
E4M3 = mybir.dt.float8_e4m3fn_x4
E2M1 = mybir.dt.float4_e2m1fn_x4
ACT = mybir.ActivationFunctionType
ALU = mybir.AluOpType

P = 128
PASSES = 2
HALF = S // 2
KIB = 1024
SHARE = 768
LAST_SHARE = 832
SHARE_BEHIND_QUANTISE = 896


def tile_list_baggage_density_cues_kernel(
    tc, tab_words, tab_scales, offs, wa, wb_words, wb_scales, gain, wc, offs2, wgo, out
):
    nc = tc.nc
    with ExitStack() as ctx:
        lists = ctx.enter_context(tc.tile_pool(name="lists", bufs=1))
        arena = ctx.enter_context(tc.tile_pool(name="arena", bufs=1))
        keep = ctx.enter_context(tc.tile_pool(name="keep", bufs=1))
        banks = ctx.enter_context(tc.psum_pool(name="banks", bufs=1))
        taken = []

        def take_bank(k):
            taken.append(k)
            return banks.tile([P, HALF], F32, name=f"bank{len(taken)}", offset=2048 * k)

        def held(name, shape, dtype):
            return keep.tile(shape, dtype, name=name, align_bytes=64)

        def placed(name, kib, shape, dtype):
            return arena.tile(shape, dtype, name=name, offset=int(kib * KIB), align_bytes=64)

        pick = lists.tile([P, S // 16], U16, name="pick")
        place = lists.tile([P, S // 16], U16, name="place")

        tscale = placed("tscale", 7, [P, T], U8)
        wbs_raw = held("wbs_raw", [P, PASSES, H // 4], U32)
        gain_rows = held("gain_rows", [P, 512], F32)
        planes = [held(f"planes{half}", [P, PASSES, HALF], U8) for half in range(2)]
        pages = {}

        def clear(i, kib):
            pages[i] = placed(f"page{i}", kib, [P, T2], F32)
            nc.gpsimd.memset(pages[i][:].bitcast(I32), 0)

        def clear_on_one_port(words):
            count = words.shape[1]
            nc.vector.memset(words[:, 0 : count // 2 - 1], 0)
            nc.vector.memset(words[:, count // 2 - 1 :], 0)

        nc.gpsimd.memset(tscale[:].bitcast(I32), 0)
        clear_on_one_port(gain_rows[:].bitcast(I32))
        clear_on_one_port(wbs_raw[:].rearrange("p a c -> p (a c)").bitcast(I32))
        for plane in planes:
            clear_on_one_port(plane[:].rearrange("p a c -> p (a c)").bitcast(I32))
        identity = held("identity", [P, P], F32)
        make_identity(nc, identity[:])
        pages[1] = placed("page1", 124, [P, T2], F32)
        nc.gpsimd.memset(pages[1][:, 0:1280].bitcast(I32), 0)
        clear_on_one_port(pages[1][:, 1280:].bitcast(I32))

        twords = [placed("twords0", 140, [P, T], U32), placed("twords1", 24, [P, T], U32)]

        def load_table(a, c0=0, c1=T):
            nc.sync.dma_start(
                out=twords[a][:, c0:c1].bitcast(I32),
                in_=tab_words[a].rearrange("p t i -> p (t i)").bitcast(I32)[:, c0:c1],
            )

        nc.sync.dma_start(pick[:], offs)
        load_table(0, 0, T // 4)
        nc.sync.dma_start(
            out=tscale[0:P:4, :].bitcast(I32), in_=tab_scales.bitcast(I32).rearrange("a q t -> q a t")
        )
        load_table(0, T // 4, T)
        wbw_raw, wbw = {}, {}

        def load_wb(b, kib):
            wbw_raw[b] = placed(f"wbw_raw{b}", kib, [P, PASSES, 256], U32)
            nc.sync.dma_start(
                out=wbw_raw[b][:].bitcast(I32),
                in_=wb_words.bitcast(I32)[:, :, 256 * b : 256 * (b + 1)].rearrange("a p c -> p a c"),
            )

        def order_wb(b):
            wbw[b] = held(f"wbw{b}", [P, PASSES, 256], U32)
            nc.scalar.copy(
                wbw[b][:].rearrange("p a (t m u) -> p a t m u", t=4, u=2),
                wbw_raw[b][:].rearrange("p a (m t u) -> p a t m u", t=4, u=2),
            )

        load_wb(0, 163)
        nc.sync.dma_start(out=gain_rows[0:PASSES, :], in_=gain.rearrange("(b c) -> b c", b=PASSES))
        for d in range(4):
            nc.sync.dma_start(
                out=wbs_raw[32 * d : 32 * d + 4, :, :].bitcast(I32),
                in_=wb_scales.bitcast(I32)[:, 4 * d : 4 * d + 4, :].rearrange("a r c -> r a c"),
            )
        load_table(1)
        load_wb(1, 166)

        order_wb(0)
        wb_planes = placed("wb_planes", 162, [P, PASSES, H // 4], U32)
        nc.scalar.copy(
            wb_planes[:].rearrange("p a (t m) -> p a t m", t=4),
            wbs_raw[:].rearrange("p a (m t) -> p a t m", t=4),
        )
        gains = banks.tile([P, 4, P], F32, name="gains", offset=2048 * 7)
        gain_dealt = placed("gain_dealt", 164, [P, 512], F32)
        nc.scalar.copy(
            gain_dealt[:].rearrange("p (t m u) -> p t m u", t=4, u=4),
            gain_rows[:].rearrange("p (m t u) -> p t m u", t=4, u=4),
        )
        for t in range(4):
            nc.tensor.transpose(gains[:, t, :], gain_dealt[:, P * t : P * (t + 1)], identity[:])
        order_wb(1)
        last_gains = held("last_gains", [P, 4], F32)
        nc.scalar.copy(last_gains[:], gains[:, :, 1:2].rearrange("p t o -> p (t o)"))

        gscale = [held(f"gscale{half}", [P, HALF], U8) for half in range(2)]

        def move_planes(half):
            for d in range(4):
                nc.sync.dma_start(
                    out=planes[half][32 * d : 32 * d + 4, :, :].rearrange("p a c -> p (a c)").bitcast(I32),
                    in_=gscale[half][32 * d : 32 * (d + 1) : 4, :].bitcast(I32),
                )

        for half in range(2):
            nc.vector.tensor_copy(gscale[half][:], tscale[:].indirect(pick[:, 32 * half : 32 * (half + 1)]))
        move_planes(0)

        wa_raw, wa_q, wa_s = {}, {}, {}

        def load_wa(a, b):
            wa_raw[a, b] = placed(f"wa_raw{a}{b}", (0, 8, 166, 24)[a + 2 * b], [P, 4, 512], F32)
            nc.sync.dma_start(
                out=wa_raw[a, b][:],
                in_=wa[512 * a : 512 * (a + 1), 512 * b : 512 * (b + 1)].rearrange("(p i) c -> p i c", i=4),
            )

        def quantise_wa(a, b):
            rounded = placed(f"wa_bf{a}{b}", (32, 36, 40, 50)[a + 2 * b], [P, 2048], BF16)
            for t in (0, 2):
                nc.vector.tensor_copy(
                    rounded[:].rearrange("p (t m u i) -> p t m i u", t=4, u=4, i=4)[:, t : t + 2],
                    wa_raw[a, b][:].rearrange("p i (m t u) -> p t m i u", t=4, u=4)[:, t : t + 2],
                )
            wa_q[a, b] = held(f"wa_q{a}{b}", [P, 512], U32)
            wa_s[a, b] = held(f"wa_s{a}{b}", [P, 512], U8)
            for c in (0, 256):
                nc.vector.quantize_mx(
                    out=wa_q[a, b][:, c : c + 256].bitcast(E4M3),
                    scales=wa_s[a, b][:, c : c + 256],
                    in_=rounded[:, 4 * c : 4 * c + 1024],
                )

        vwords = {}

        def gather(a, half, tile):
            vwords[a, half] = tile
            nc.vector.tensor_copy(tile[:], twords[a][:].indirect(pick[:, 32 * half : 32 * (half + 1)]))

        wc_raw, wc_bf, wc_q, wc_s = {}, {}, {}, {}

        def load_wc(b):
            wc_raw[b] = placed(f"wc_raw{b}", 8 * b, [P, 4, N], F32)
            rows = wc[512 * b : 512 * (b + 1), :].rearrange("(m t u) n -> t m u n", t=4, u=4)
            for t in range(4):
                nc.sync.dma_start(out=wc_raw[b][:, t, :], in_=rows[t])

        def round_wc(pair, b, copy=nc.scalar.copy, q0=0, q1=P):
            if b == 0:
                wc_bf[pair] = placed(f"wc_bf{pair}", (108, 151)[pair], [P, PASSES, 1024], BF16)
            copy(
                wc_bf[pair][:, b, :].rearrange("p (e q t) -> p q t e", e=2, t=4)[:, q0:q1],
                wc_raw[b][:].rearrange("p t (q i) -> p q t i", i=4)[:, q0:q1, :, 2 * pair : 2 * pair + 2],
            )

        def quantise_wc(pair):
            wc_q[pair] = held(f"wc_q{pair}", [P, 512], U32)
            wc_s[pair] = placed(f"wc_s{pair}", (144, 18)[pair], [P, 512], U8)
            nc.vector.quantize_mx(
                out=wc_q[pair][:].bitcast(E4M3),
                scales=wc_s[pair][:],
                in_=wc_bf[pair][:].rearrange("p b c -> p (b c)"),
            )

        def operands(reading, a, b, t):
            if reading == "a":
                cols = slice(P * t, P * (t + 1))
                return wa_q[a, b][:, cols].bitcast(E4M3), wa_s[a, b][:, cols]
            col = t * 256 + b * P
            codes = wbw[b][:].bitcast(U8)[:, a, 2 * P * t : 2 * P * (t + 1)]
            return codes.bitcast(E2M1), wb_planes[:].bitcast(U8)[:, a, col : col + P]

        def multiply(bank, reading, b, t, j0, width):
            half, c0 = divmod(j0, HALF)
            for a in range(PASSES):
                codes, scales = operands(reading, a, b, t)
                nc.tensor.matmul_mx(
                    out=bank,
                    lhsT=codes,
                    lhsT_scale=scales,
                    rhs=vwords[a, half][:, c0 : c0 + width].bitcast(E4M3),
                    rhs_scale=planes[half][:, a, c0 : c0 + width],
                    start=(a == 0),
                    stop=(a == PASSES - 1),
                )

        exps, difference, hb, h_q, h_s = {}, {}, {}, {}, {}
        exps_at = {"a": (60, 76, 92, 132), "b": (68, 84, 100, 116)}

        def exp_tile(reading, b, half):
            exps[reading, b, half] = placed(
                f"e{reading}{b}{half}", exps_at[reading][b + 2 * half], [P, 4 * HALF], F32
            )
            return exps[reading, b, half]

        def read(reading, b, half, ring, first=0):
            tile = exps[reading, b, half] if first else exp_tile(reading, b, half)
            for t, k in enumerate(ring, first):
                bank = take_bank(k)
                multiply(bank[:], reading, b, t, HALF * half, HALF)
                nc.scalar.activation(tile[:, HALF * t : HALF * (t + 1)], bank[:], ACT.Exp)

        def subtract(engine, b, half, c0, c1, kib=None):
            if kib is not None:
                difference[b, half] = placed(f"difference{b}{half}", kib, [P, 4 * HALF], F32)
            views = (difference[b, half], exps["a", b, half], exps["b", b, half])
            engine.tensor_tensor(*[view[:, c0:c1] for view in views], ALU.subtract)

        def subtract_first(kib):
            difference[0, 0] = placed("difference00", kib, [P, 4 * HALF], F32)
            views = (difference[0, 0], exps["a", 0, 0], exps["b", 0, 0])
            for j0 in (0, HALF // 2):
                nc.vector.tensor_tensor(
                    *[view[:].rearrange("p (t j) -> p t j", t=4)[:, :, j0 : j0 + HALF // 2] for view in views],
                    ALU.subtract,
                )

        def scale(b, half, kib, parts=1):
            hb[b, half] = placed(f"hb{b}{half}", kib, [P, 4 * HALF], BF16)
            fours = HALF // 4 // parts
            for c0 in range(0, HALF // 4, fours):
                nc.vector.tensor_tensor(
                    hb[b, half][:].rearrange("p (c i t) -> p c t i", i=4, t=4)[:, c0 : c0 + fours],
                    difference[b, half][:].rearrange("p (t c i) -> p c t i", t=4, i=4)[:, c0 : c0 + fours],
                    gains[:, :, b : b + 1].unsqueeze(1).to_broadcast([P, fours, 4, 4]),
                    ALU.mult,
                )

        def subtract_last(c0, c1, kib):
            difference[1, 1, c0] = placed(f"difference11_{c0}", kib, [P, c1 - c0], F32)
            nc.gpsimd.tensor_tensor(
                difference[1, 1, c0][:], exps["a", 1, 1][:, c0:c1], exps["b", 1, 1][:, c0:c1], ALU.subtract
            )

        def scale_last(start, c0, c1):
            t = c0 // HALF
            nc.scalar.activation(
                scaled[:, c0:c1],
                difference[1, 1, start][:, c0 - start : c1 - start],
                ACT.Copy,
                scale=last_gains[:, t : t + 1],
            )

        def weave(kib):
            hb[1, 1] = placed("hb11", kib, [P, 4 * HALF], BF16)
            nc.scalar.copy(
                hb[1, 1][:].rearrange("p (c i t) -> p c t i", i=4, t=4),
                scaled[:].rearrange("p (t c i) -> p c t i", t=4, i=4),
            )

        def quantise_h(b, half, kib=None):
            h_q[b, half] = held(f"h_q{b}{half}", [P, HALF], U32)
            name = f"h_s{b}{half}"
            h_s[b, half] = held(name, [P, HALF], U8) if kib is None else placed(name, kib, [P, HALF], U8)
            nc.vector.quantize_mx(out=h_q[b, half][:].bitcast(E4M3), scales=h_s[b, half][:], in_=hb[b, half][:])

        squares, ys = {}, {}

        def mix(i, half, kib):
            pair, e = divmod(i, 2)
            bank = take_bank((4, 5, 6)[len(squares) % 3])
            for b in range(PASSES):
                col = 256 * b + P * e
                nc.tensor.matmul_mx(
                    out=bank[:],
                    lhsT=wc_q[pair][:, col : col + P].bitcast(E4M3),
                    lhsT_scale=wc_s[pair][:, col : col + P],
                    rhs=h_q[b, half][:].bitcast(E4M3),
                    rhs_scale=h_s[b, half][:],
                    start=(b == 0),
                    stop=(b == PASSES - 1),
                )
            squares[i, half] = placed(f"square{i}{half}", kib, [P, HALF], F32)
            nc.scalar.activation(squares[i, half][:], bank[:], ACT.Square)

        def logarithm(i, half, into=None):
            ys[i, half] = squares[i, half][:] if into is None else into
            nc.scalar.activation(ys[i, half], squares[i, half][:], ACT.Ln, bias=1.0)

        rows = out.rearrange("(p i) t -> i p t", i=4)

        def slots(i, half):
            return pages[i][:].indirect(place[:, 32 * half : 32 * (half + 1)])

        def scatter(i, half):
            nc.vector.tensor_tensor(
                slots(i, half), ys[i, half], weights[:, HALF * half : HALF * (half + 1)], ALU.mult
            )

        load_wa(0, 0)
        load_wa(1, 0)
        move_planes(1)
        gather(0, 0, held("vwords00", [P, HALF], U32))
        gather(0, 1, held("vwords01", [P, HALF], U32))
        load_wa(0, 1)
        gather(1, 0, held("vwords10", [P, HALF], U32))
        read("b", 0, 0, (0, 1, 2, 3))
        gather(1, 1, placed("vwords11", 174, [P, HALF], U32))
        load_wa(1, 1)
        read("b", 1, 0, (0, 1, 2, 3))
        quantise_wa(0, 0)
        load_wc(0)
        quantise_wa(1, 0)
        load_wc(1)
        read("b", 0, 1, (0,))
        read("a", 0, 0, (4, 5, 6, 1))
        quantise_wa(0, 1)
        nc.sync.dma_start(place[:], offs2)
        weights = placed("weights", 36, [P, S], F32)
        nc.sync.dma_start(out=weights[:], in_=wgo)
        quantise_wa(1, 1)
        late = (2, 3, 0, 1)
        read("b", 0, 1, (4, 5, 6), first=1)
        read("a", 1, 0, late)
        round_wc(0, 0)
        read("a", 0, 1, late)
        round_wc(0, 1, q0=P // 2)
        for t in range(4):
            read("b", 1, 1, (late[2 * t % 4],), first=t)
            read("a", 1, 1, (late[(2 * t + 1) % 4],), first=t)

        clear(0, 44)
        subtract_first(52)
        subtract(nc.gpsimd, 1, 0, 0, SHARE, exps_at["b"][0])
        scale(0, 0, 60, parts=2)
        round_wc(0, 1, nc.vector.tensor_copy, 0, P // 2)
        subtract(nc.vector, 1, 0, SHARE, 2048)
        subtract(nc.gpsimd, 0, 1, 0, SHARE_BEHIND_QUANTISE, exps_at["b"][1])
        quantise_h(0, 0)
        scale(1, 0, 64)
        quantise_wc(0)
        quantise_h(1, 0)
        subtract(nc.vector, 0, 1, SHARE_BEHIND_QUANTISE, 2048)
        subtract_last(0, LAST_SHARE, 104)
        scale(0, 1, 140)

        mix(0, 0, 150)
        first_y = placed("y00", 174, [P, HALF], F32)
        weighted = placed("weighted", 18, [P, HALF], F32)
        for j0 in (0, HALF // 2):
            cols = slice(j0, j0 + HALF // 2)
            nc.scalar.activation(first_y[:, cols], squares[0, 0][:, cols], ACT.Ln, bias=1.0)
            nc.vector.tensor_tensor(weighted[:, cols], first_y[:, cols], weights[:, cols], ALU.mult)
        quantise_h(0, 1, 175)
        nc.vector.tensor_copy(slots(0, 0), weighted[:])
        subtract_last(LAST_SHARE, 4 * HALF, 170)
        round_wc(1, 0)
        round_wc(1, 1)
        mix(1, 0, 149)
        logarithm(1, 0, placed("y10", 16, [P, HALF], F32)[:])
        quantise_wc(1)
        clear(2, 145)
        clear(3, 153)
        scatter(1, 0)
        scaled = placed("scaled", 108, [P, 4 * HALF], F32)
        for start, c0, c1 in ((0, 0, HALF), (0, HALF, LAST_SHARE), (LAST_SHARE, LAST_SHARE, 2 * HALF), (LAST_SHARE, 2 * HALF, 3 * HALF), (LAST_SHARE, 3 * HALF, 4 * HALF)):
            scale_last(start, c0, c1)
        mix(2, 0, 170)
        logarithm(2, 0, placed("y20", 26, [P, HALF], F32)[:])
        scatter(2, 0)
        weave(167)
        quantise_h(1, 1)
        mix(3, 0, 108)
        logarithm(3, 0)
        scatter(3, 0)
        for i in range(4):
            mix(i, 1, 68 + 2 * i)
            logarithm(i, 1)
            scatter(i, 1)
            nc.sync.dma_start(out=rows[i], in_=pages[i][:])
